import numpy as np
import ml_dtypes


def mxq(x, axis, fmt="e4m3"):
    dtype, down = {"e4m3": (ml_dtypes.float8_e4m3fn, 7), "e5m2": (ml_dtypes.float8_e5m2, 14)}[fmt]
    v = np.moveaxis(np.asarray(x, np.float32).astype(ml_dtypes.bfloat16).astype(np.float64), axis, -1)
    blocks = v.reshape(v.shape[:-1] + (-1, 32))
    amax = np.abs(blocks).max(-1, keepdims=True)
    byte = np.maximum(np.where(amax > 0, np.frexp(amax)[1] - 1 + 127, 0) - down, 1)
    scale = np.exp2(byte - 127.0)
    codes = (blocks / scale).astype(np.float32).astype(dtype).astype(np.float64)
    return np.moveaxis((codes * scale).reshape(v.shape), -1, axis)


WIDE = False


def mx_kscale(k):
    if not WIDE:
        return np.ones(k)
    levels = np.array([10, -10, 5, -5, 0])
    if k % 512:
        return np.exp2(np.random.permutation(np.resize(levels, k // 32))).repeat(32)
    a = np.empty((k // 512, 16))
    for p in range(k // 512):
        a[p, :8] = np.random.permutation(np.resize(levels, 8))
        for g in range(8):
            far = levels[np.abs(levels - a[p, g]) >= 10]
            a[p, g + 8] = far[np.random.randint(len(far))]
    return np.exp2(a.ravel()).repeat(32)


def f64(x):
    return np.asarray(x).astype(np.float64)


def striped(idx):
    return np.tile(idx.reshape(-1, 16).T, (8, 1)).astype(np.uint16)


def unstriped(offs):
    return offs[:16].T.reshape(-1).astype(np.int64)


E2M1 = np.array([0.0, 0.5, 1.0, 1.5, 2.0, 3.0, 4.0, 6.0, -0.0, -0.5, -1.0, -1.5, -2.0, -3.0, -4.0, -6.0])


def pack_weight(w, fmt):
    k, n = w.shape
    w = f64(np.asarray(w, np.float32).astype(ml_dtypes.bfloat16)).reshape(k // 32, 32, n)
    amax = np.abs(w).max(1)
    if fmt == "e4m3":
        byte = np.frexp(amax)[1] - 1 + 127 - 7
    else:
        mant, ex = np.frexp(amax / 6.0)
        byte = np.where(mant > 0.5, ex, ex - 1) + 127
    byte = np.clip(np.where(amax > 0, byte, 1), 1, 254)
    scaled = (w * np.exp2(127.0 - byte)[:, None, :]).reshape(k, n).astype(np.float32)
    by_word = np.ascontiguousarray(scaled.reshape(k // 512, 128, 4, n).transpose(0, 1, 3, 2))
    if fmt == "e4m3":
        words = by_word.astype(ml_dtypes.float8_e4m3fn).view(np.uint8)
    else:
        c = by_word.astype(ml_dtypes.float4_e2m1fn).view(np.uint8) & 0xF
        words = (c[..., 0::2] | (c[..., 1::2] << 4)).reshape(k // 512, 128, 2 * n)
    return np.ascontiguousarray(words), np.ascontiguousarray(byte.astype(np.uint8).reshape(k // 512, 16, n))


def unpack_weight(words, scales, fmt):
    g, _, n = scales.shape
    words = np.ascontiguousarray(words).reshape(g, 128, n, -1)
    if fmt == "e4m3":
        vals = words.view(ml_dtypes.float8_e4m3fn).astype(np.float64)
    else:
        nib = np.empty((g, 128, n, 4), np.uint8)
        nib[..., 0::2] = words & 0xF
        nib[..., 1::2] = words >> 4
        vals = E2M1[nib]
    vals = vals * np.repeat(np.exp2(scales.astype(np.float64) - 127.0), 8, axis=1)[..., None]
    return vals.transpose(0, 1, 3, 2).reshape(g * 512, n)


def gelu(v):
    return 0.5 * v * (1.0 + np.tanh(np.sqrt(2.0 / np.pi) * (v + 0.044715 * v**3)))


K, T, S, T2, P, H, N = 1024, 2048, 512, 1024, 512, 1024, 512

def setup_inputs():
    n = np.random.standard_normal
    ks = mx_kscale(K)[:, None]
    u = mx_kscale(H)[:, None]
    tab_words, tab_scales = pack_weight(n((K, T)) * ks, "e4m3")
    w2_words, w2_scales = pack_weight(0.6 * n((K, H)) / np.sqrt(K) / ks, "e2m1")
    w4_words, w4_scales = pack_weight(3.0 * n((H, N)) / np.sqrt(H) / u, "e4m3")
    temp = np.random.uniform(0.4, 1.6, H)
    gain = np.random.choice([-1.0, 1.0], H) * 3.0 * temp * u[:, 0]
    return {
        "tab_words": tab_words, "tab_scales": tab_scales,
        "offs": striped(np.random.permutation(T)[:S]),
        "w1": (0.8 * n((K, H)) / np.sqrt(K) / ks).astype(np.float32),
        "w2_words": w2_words, "w2_scales": w2_scales,
        "edit": np.random.uniform(-1.0, 1.0, (H, S)).astype(np.float32),
        "page0": (0.8 * n((H, T2))).astype(np.float32),
        "wgs": np.exp(0.3 * n((128, S))).astype(np.float32),
        "offs2": striped(np.random.permutation(T2)[:S]),
        "offs3": striped(np.random.permutation(T2)[:P]),
        "temp": temp.astype(np.float32),
        "gain": gain.astype(np.float32),
        "w3": (3.0 * n((H, N)) / np.sqrt(H) / u).astype(np.float32),
        "w4_words": w4_words, "w4_scales": w4_scales,
        "audit": n((N, P)).astype(np.float32),
    }

def reference(tab_words, tab_scales, offs, w1, w2_words, w2_scales, edit, page0, wgs,
              offs2, offs3, temp, gain, w3, w4_words, w4_scales, audit):
    v = unpack_weight(tab_words, tab_scales, "e4m3")[:, unstriped(offs)]
    h = f64(edit) * (mxq(f64(w1), 0, "e4m3").T @ v) + (unpack_weight(w2_words, w2_scales, "e2m1").T @ v)
    page = f64(page0).copy()
    page[:, unstriped(offs2)] = np.tile(f64(wgs), (H // 128, 1)) * h
    top = page.max(axis=1)
    x = np.exp(f64(temp)[:, None] * (page[:, unstriped(offs3)] - top[:, None]))
    z = mxq(f64(gain)[:, None] * x, 0, "e4m3")
    return f64(audit) * (mxq(f64(w3), 0, "e4m3").T @ z) + (unpack_weight(w4_words, w4_scales, "e4m3").T @ z)

@@ -1,0 +1,410 @@
+from contextlib import ExitStack
+
+import concourse.mybir as mybir
+
+K, T, S, T2, PM, H, N = 1024, 2048, 512, 1024, 512, 1024, 512
+FLOPS = 2 * 2 * K * H * S + 2 * 2 * H * N * PM
+
+F32 = mybir.dt.float32
+BF16 = mybir.dt.bfloat16
+I32 = mybir.dt.int32
+U32 = mybir.dt.uint32
+U16 = mybir.dt.uint16
+U8 = mybir.dt.uint8
+FP8X4 = mybir.dt.float8_e4m3fn_x4
+FP4X4 = mybir.dt.float4_e2m1fn_x4
+ALU = mybir.AluOpType
+ACT = mybir.ActivationFunctionType
+
+P = 128
+PACK = 4
+PASS = P * PACK
+PATHS = "VVVVVVVV"
+TAIL_G = 2
+
+
+def tile_list_repair_error_scores_kernel(
+    tc, tab_words, tab_scales, offs, w1, w2_words, w2_scales, edit, page0, wgs,
+    offs2, offs3, temp, gain, w3, w4_words, w4_scales, audit, out,
+):
+    nc = tc.nc
+    kp = K // PASS
+    rp = H // PASS
+    tiles = H // P
+    ntiles = N // P
+
+    with ExitStack() as ctx:
+        lists = ctx.enter_context(tc.tile_pool(name="lists", bufs=1))
+        keep = ctx.enter_context(tc.tile_pool(name="keep", bufs=1))
+        ring = ctx.enter_context(tc.tile_pool(name="ring", bufs=3))
+        psum = ctx.enter_context(tc.psum_pool(name="psum", bufs=1))
+
+        def held(shape, dtype, name):
+            return keep.tile(shape, dtype, name=name, align_bytes=64)
+
+        idx = lists.tile([P, S // 16], U16, name="idx")
+        idx2 = lists.tile([P, S // 16], U16, name="idx2")
+        idx3 = lists.tile([P, PM // 16], U16, name="idx3")
+
+        tab_s = held([P, kp, T], U8, "tab_s")
+        w2_s = held([P, kp, H], U8, "w2_s")
+        w4_s = held([P, rp, N], U8, "w4_s")
+        nc.vector.memset(tab_s[:].rearrange("p a t -> p (a t)").bitcast(I32), 0)
+        nc.gpsimd.memset(w2_s[:].rearrange("p a t -> p (a t)").bitcast(I32), 0)
+        nc.vector.memset(w4_s[:].rearrange("p a t -> p (a t)").bitcast(I32), 0)
+
+        def load_scales(queue, tile, src):
+            for q in range(4):
+                queue.dma_start(
+                    out=tile[32 * q : 32 * q + 4].bitcast(I32),
+                    in_=src[:, 4 * q : 4 * q + 4, :].rearrange("a r c -> r a c").bitcast(I32),
+                )
+
+        def rows_of(src, u):
+            if u < PACK:
+                return src[u * P : (u + 1) * P, :]
+            return src[PASS:, :].rearrange("(p i) c -> i p c", i=PACK)[u - PACK]
+
+        w1_raw, w2_w, tab_w, w3_raw, edit_t, page, wgs_t, audit_t = {}, {}, {}, {}, {}, {}, {}, {}
+
+        def load_w1(u0, u1):
+            width = (u1 - u0) * P
+            for a in range(kp):
+                if width == PASS:
+                    raw = ring.tile([P, PACK, PASS], F32, name="raw", bufs=3)
+                else:
+                    raw = held([P, PACK, width], F32, f"w1_raw{a}{u0}")
+                w1_raw[a, u0] = raw
+                rows = w1[a * PASS : (a + 1) * PASS, u0 * P : u1 * P]
+                nc.sync.dma_start(out=raw[:], in_=rows.rearrange("(p j) c -> p j c", j=PACK))
+
+        def load_w2(b):
+            w2_w[b] = held([P, kp, 2 * PASS], U8, f"w2_w{b}")
+            src = w2_words[:, :, 2 * b * PASS : 2 * (b + 1) * PASS]
+            nc.sync.dma_start(out=w2_w[b][:].bitcast(I32), in_=src.rearrange("a p c -> p a c").bitcast(I32))
+
+        def load_tab(a):
+            tab_w[a] = held([P, T], U32, f"tab_w{a}")
+            nc.sync.dma_start(
+                out=tab_w[a][:].bitcast(I32),
+                in_=tab_words[a].rearrange("p t i -> p (t i)").bitcast(I32),
+            )
+
+        def load_edit(u):
+            edit_t[u] = held([P, S], F32, f"edit{u}")
+            nc.sync.dma_start(out=edit_t[u][:], in_=rows_of(edit, u))
+
+        def load_page(u):
+            page[u] = held([P, T2], F32, f"page{u}")
+            nc.sync.dma_start(out=page[u][:], in_=rows_of(page0, u))
+
+        def load_wgs_dealt():
+            tile = held([P, PACK, S], F32, "wgs_dealt")
+            for q in (0, 2, 1, 3):
+                nc.sync.dma_start(out=tile[32 * q : 32 * q + 32], in_=wgs.rearrange("(q i) j -> q i j", i=PACK))
+            for i in range(PACK):
+                wgs_t[PACK + i] = tile[:, i, :]
+
+        def load_w3(b):
+            w3_raw[b] = ring.tile([P, PACK, N], F32, name="raw", bufs=3)
+            nc.sync.dma_start(
+                out=w3_raw[b][:],
+                in_=w3[b * PASS : (b + 1) * PASS, :].rearrange("(p j) c -> p j c", j=PACK),
+            )
+
+        def load_audit(n0):
+            tile = held([P, 2, PM], F32, f"audit{n0}")
+            nc.sync.dma_start(out=tile[:], in_=audit[n0 * P : (n0 + 2) * P, :].rearrange("(n p) m -> p n m", p=P))
+            audit_t[n0], audit_t[n0 + 1] = tile[:, 0, :], tile[:, 1, :]
+
+        def load_per_row(vec, name):
+            first = held([P, PACK], F32, name + "0")
+            second = held([P, PACK], F32, name + "1")
+            with nc.allow_non_contiguous_dma(reason="one value a partition"):
+                nc.sync.dma_start(out=first[:], in_=vec[:PASS].rearrange("(u p) -> p u", p=P))
+            nc.sync.dma_start(out=second[:], in_=vec[PASS:].rearrange("(p i) -> p i", i=PACK))
+            return first, second
+
+        wgs_plain = held([P, S], F32, "wgs_plain")
+        w4_w = held([P, rp, N], U32, "w4_w")
+        for u in range(PACK):
+            wgs_t[u] = wgs_plain[:]
+
+        nc.sync.dma_start(idx[:], offs)
+        load_w1(0, 1)
+        load_scales(nc.sync, tab_s, tab_scales)
+        load_tab(0)
+        load_tab(1)
+        load_scales(nc.sync, w2_s, w2_scales)
+        load_w2(0)
+        load_edit(0)
+        load_w1(1, 2)
+        nc.sync.dma_start(out=wgs_plain[:], in_=wgs)
+        nc.sync.dma_start(idx2[:], offs2)
+        load_page(0)
+        load_edit(1)
+        temp_t = load_per_row(temp, "temp")
+        load_w1(2, 4)
+        load_page(1)
+        load_edit(2)
+        nc.sync.dma_start(idx3[:], offs3)
+        gain_t = load_per_row(gain, "gain")
+        load_w1(PACK, tiles)
+        load_page(2)
+        load_edit(3)
+        load_w2(1)
+        load_page(3)
+        load_edit(4)
+        load_wgs_dealt()
+        load_page(4)
+        load_edit(5)
+        load_w3(0)
+        load_page(5)
+        load_edit(6)
+        load_w3(1)
+        load_page(6)
+        load_edit(7)
+        load_scales(nc.sync, w4_s, w4_scales)
+        nc.sync.dma_start(
+            out=w4_w[:].bitcast(I32),
+            in_=w4_words.rearrange("a p c i -> p a (c i)").bitcast(I32),
+        )
+        load_page(7)
+        load_audit(0)
+        load_audit(2)
+
+        neg_temp = [held([P, PACK], F32, f"neg_temp{b}") for b in range(rp)]
+        for b in range(rp):
+            nc.scalar.mul(neg_temp[b][:], temp_t[b][:], -1.0)
+
+        def column(pair, u):
+            return pair[u // PACK][:, u % PACK : u % PACK + 1]
+
+        v_s, v_w = {}, {}
+
+        def gather_scales(a):
+            v_s[a] = held([P, S], U8, f"v_s{a}")
+            nc.vector.tensor_copy(v_s[a][:], tab_s[:, a, :].indirect(idx[:]))
+
+        def gather_words(a):
+            v_w[a] = held([P, S], U32, f"v_w{a}")
+            nc.vector.tensor_copy(v_w[a][:], tab_w[a][:].indirect(idx[:]))
+
+        def quantise(grouped, width, name, codes=None):
+            if codes is None:
+                codes = held([P, width], U32, name + "_c")
+            scales = held([P, width], U8, name + "_s")
+            nc.vector.quantize_mx(out=codes[:].bitcast(FP8X4), scales=scales[:], in_=grouped)
+            return codes, scales
+
+        def interleave(dst, src):
+            nc.scalar.copy(
+                out=dst.rearrange("p (c e j) -> p c j e", e=4, j=PACK),
+                in_=src.rearrange("p j (c e) -> p c j e", e=4),
+            )
+
+        w1_q = {}
+
+        def prepare_w1_plain(u0, u1):
+            width = (u1 - u0) * P
+            grouped = ring.tile([P, kp, width * PACK], BF16, name="grouped", align_bytes=64)
+            for a in range(kp):
+                interleave(grouped[:, a, :], w1_raw[a, u0][:])
+            codes, scales = quantise(grouped[:].rearrange("p a c -> p (a c)"), kp * width, f"w1q{u0}")
+            for a in range(kp):
+                for u in range(u0, u1):
+                    cols = slice(a * width + (u - u0) * P, a * width + (u - u0 + 1) * P)
+                    w1_q[a, u] = (codes[:, cols], scales[:, cols])
+
+        def prepare_w1_dealt(a, slot):
+            grouped = ring.tile([P, PASS * PACK], BF16, name="grouped", align_bytes=64)
+            nc.scalar.copy(
+                out=grouped[:].rearrange("p (i m j) -> p m j i", i=PACK, j=PACK),
+                in_=w1_raw[a, PACK][:].rearrange("p j (m i) -> p m j i", i=PACK),
+            )
+            codes, scales = quantise(grouped[:], PASS, f"w1q_dealt{a}", slot)
+            for i in range(PACK):
+                w1_q[a, PACK + i] = (codes[:, i * P : (i + 1) * P], scales[:, i * P : (i + 1) * P])
+
+        w2_wd = held([P, kp, 2 * PASS], U8, "w2_wd")
+        w2_sd = {}
+
+        def deal_w2_scales(u):
+            w2_sd[1] = held([P, kp, PASS], U8, f"ready{u}")
+            nc.vector.tensor_copy(
+                out=w2_sd[1][:].rearrange("p a (i m) -> p a i m", i=PACK),
+                in_=w2_s[:, :, PASS:].rearrange("p a (m i) -> p a i m", i=PACK),
+            )
+
+        def deal_w2_words():
+            nc.scalar.copy(
+                out=w2_wd[:].bitcast(U16).rearrange("p a (i m) -> p a i m", i=PACK),
+                in_=w2_w[1][:].bitcast(U16).rearrange("p a (m i) -> p a i m", i=PACK),
+            )
+
+        bias = held([P, tiles], F32, "bias")
+        scaled = held([P, T2], F32, "scaled")
+        z_plain = held([P, PACK, PM], F32, "z_plain")
+        z_last = held([P, PM, PACK], BF16, "z_last")
+        banks, z_q, w3_q, gated, ready = {}, {}, {}, {}, {}
+
+        def first_products(u):
+            i = u % PACK
+            words, bytes_ = (w2_w[0], w2_s) if u < PACK else (w2_wd, w2_sd[1])
+            p1 = psum.tile([P, S], F32, name=f"bank{2 * i}")
+            p2 = psum.tile([P, S], F32, name=f"bank{2 * i + 1}")
+            for a in range(kp):
+                codes, scales = w1_q[a, u]
+                nc.tensor.matmul_mx(
+                    out=p1[:], lhsT=codes.bitcast(FP8X4), lhsT_scale=scales,
+                    rhs=v_w[a][:].bitcast(FP8X4), rhs_scale=v_s[a][:], start=(a == 0), stop=(a == kp - 1),
+                )
+            for a in range(kp):
+                nc.tensor.matmul_mx(
+                    out=p2[:], lhsT=words[:, a, 2 * i * P : 2 * (i + 1) * P].bitcast(FP4X4),
+                    lhsT_scale=bytes_[:, a, i * P : (i + 1) * P],
+                    rhs=v_w[a][:].bitcast(FP8X4), rhs_scale=v_s[a][:], start=(a == 0), stop=(a == kp - 1),
+                )
+            banks[u] = (p1, p2)
+
+        def gate(u):
+            gated[u] = ring.tile([P, S], F32, name="gated", bufs=2)
+            nc.vector.tensor_tensor(out=gated[u][:], in0=banks[u][0][:], in1=edit_t[u][:], op=ALU.mult)
+
+        def after_put(u):
+            return held([P, S], U32, f"ready{u}")
+
+        def weigh(u):
+            h = held([P, S], F32, f"ready{u}") if PATHS[u] == "V" else ring.tile([P, S], F32, name="h", bufs=2)
+            if PATHS[u] == "G":
+                second = ring.tile([P, S], F32, name="second", bufs=2)
+                nc.scalar.copy(out=second[:], in_=banks[u][1][:])
+                nc.gpsimd.tensor_tensor(out=h[:], in0=second[:], in1=gated[u][:], op=ALU.add)
+            else:
+                nc.vector.tensor_tensor(out=h[:], in0=banks[u][1][:], in1=gated[u][:], op=ALU.add)
+            if PATHS[u] == "V":
+                ready[u] = h
+            else:
+                ready[u] = held([P, S], F32, f"ready{u}")
+                nc.gpsimd.tensor_tensor(out=ready[u][:], in0=h[:], in1=wgs_t[u], op=ALU.mult)
+
+        def put(u):
+            if PATHS[u] == "V":
+                nc.vector.tensor_tensor(page[u][:].indirect(idx2[:]), ready[u][:], wgs_t[u], ALU.mult)
+            else:
+                nc.vector.tensor_copy(page[u][:].indirect(idx2[:]), ready[u][:])
+
+        def row_max(u):
+            nc.vector.tensor_scalar(
+                out=scaled[:], in0=page[u][:], scalar1=column(neg_temp, u), scalar2=None,
+                op0=ALU.mult, op1=ALU.min, accum_out=bias[:, u : u + 1],
+            )
+
+        def look(u):
+            parts = 2 if u == tiles - 1 else 1
+            width = PM // parts
+            if u >= tiles - 2:
+                whole = held([P, PM], F32, "planes")
+            else:
+                whole = ring.tile([P, PM], F32, name="x", bufs=2)
+            for part in range(parts):
+                x = whole[:, part * width : (part + 1) * width]
+                entries = idx3[:, part * width // 16 : (part + 1) * width // 16]
+                nc.scalar.activation(
+                    out=x, in_=page[u][:].indirect(entries), func=ACT.Exp,
+                    bias=bias[:, u : u + 1], scale=column(temp_t, u),
+                )
+                if u < PACK:
+                    nc.scalar.activation(out=z_plain[:, u, :], in_=x, func=ACT.Copy, scale=column(gain_t, u))
+                elif parts == 1:
+                    nc.scalar.activation(out=z_last[:, :, u - PACK], in_=x, func=ACT.Copy, scale=column(gain_t, u))
+                else:
+                    nc.vector.tensor_scalar(
+                        out=z_last[:, part * width : (part + 1) * width, u - PACK], in0=x,
+                        scalar1=column(gain_t, u), scalar2=None, op0=ALU.mult,
+                    )
+
+        def prepare_w3(b, slot):
+            grouped = ring.tile([P, N * PACK], BF16, name="grouped", align_bytes=64)
+            interleave(grouped[:], w3_raw[b][:])
+            w3_q[b] = quantise(grouped[:], N, f"w3q{b}", slot)
+
+        def fetch_first_z():
+            nc.sync.dma_start(out=out.rearrange("(u p) m -> p u m", p=P), in_=z_plain[:])
+            planes = held([P, PACK, PM], F32, "planes")
+            nc.sync.dma_start(out=planes[:], in_=out.rearrange("(p i) m -> p i m", i=PACK))
+            grouped = held([P, PM * PACK], BF16, "z_first")
+            interleave(grouped[:], planes[:])
+            return grouped
+
+        prepare_w1_plain(0, 1)
+        gather_scales(0)
+        gather_scales(1)
+        gather_words(0)
+        gather_words(1)
+        first_products(0)
+        prepare_w1_plain(1, 2)
+        first_products(1)
+        gate(0)
+        weigh(0)
+        for u in range(tiles):
+            put(u)
+            if u + 1 < tiles:
+                gate(u + 1)
+            row_max(u)
+            if u + 1 < tiles:
+                weigh(u + 1)
+            if u == 0:
+                prepare_w1_plain(2, 4)
+                first_products(2)
+                first_products(3)
+            if u == 1:
+                deal_w2_scales(0)
+                prepare_w1_dealt(0, after_put(1))
+            if u == 2:
+                prepare_w1_dealt(1, after_put(2))
+                deal_w2_words()
+            if 2 <= u < tiles - 2:
+                first_products(u + 2)
+            if u in (4, 5):
+                prepare_w3(u - 4, after_put(u))
+            if u == 7:
+                z_q[0] = quantise(z_first[:], PM, "z0", after_put(u))
+            look(u)
+            if u == PACK:
+                z_first = fetch_first_z()
+
+        acc = [
+            (psum.tile([P, PM], F32, name=f"bank{2 * n}"), psum.tile([P, PM], F32, name=f"bank{2 * n + 1}"))
+            for n in range(ntiles)
+        ]
+
+        def second_products(b, n):
+            cols = slice(n * P, (n + 1) * P)
+            zc, zs = z_q[b]
+            codes, scales = w3_q[b]
+            nc.tensor.matmul_mx(
+                out=acc[n][0][:], lhsT=codes[:, cols].bitcast(FP8X4), lhsT_scale=scales[:, cols],
+                rhs=zc[:].bitcast(FP8X4), rhs_scale=zs[:], start=(b == 0), stop=(b == rp - 1),
+            )
+            nc.tensor.matmul_mx(
+                out=acc[n][1][:], lhsT=w4_w[:, b, cols].bitcast(FP8X4), lhsT_scale=w4_s[:, b, cols],
+                rhs=zc[:].bitcast(FP8X4), rhs_scale=zs[:], start=(b == 0), stop=(b == rp - 1),
+            )
+
+        for n in range(ntiles):
+            second_products(0, n)
+        z_q[1] = quantise(z_last[:].rearrange("p m i -> p (m i)"), PM, "z1")
+        for n in range(ntiles):
+            second_products(1, n)
+        for n in range(ntiles):
+            audited = held([P, PM], F32, f"edit{n}")
+            nc.vector.tensor_tensor(out=audited[:], in0=acc[n][0][:], in1=audit_t[n], op=ALU.mult)
+            result = ring.tile([P, PM], F32, name="result", bufs=4)
+            if n < TAIL_G:
+                fourth = ring.tile([P, PM], F32, name="second", bufs=2)
+                nc.scalar.copy(out=fourth[:], in_=acc[n][1][:])
+                nc.gpsimd.tensor_tensor(out=result[:], in0=fourth[:], in1=audited[:], op=ALU.add)
+            else:
+                nc.vector.tensor_tensor(out=result[:], in0=acc[n][1][:], in1=audited[:], op=ALU.add)
+            nc.sync.dma_start(out=out[n * P : (n + 1) * P, :], in_=result[:])

@@ -19,7 +19,7 @@ ACT = mybir.ActivationFunctionType
 P = 128
 PACK = 4
 PASS = P * PACK
-PATHS = "VVVVVVVV"
+PATHS = "VVMGGGGG"
 TAIL_G = 2
 
 
@@ -145,32 +145,32 @@ def tile_list_repair_error_scores_kernel(
         load_edit(1)
         temp_t = load_per_row(temp, "temp")
         load_w1(2, 4)
-        load_page(1)
         load_edit(2)
+        load_edit(3)
+        load_page(1)
         nc.sync.dma_start(idx3[:], offs3)
         gain_t = load_per_row(gain, "gain")
         load_w1(PACK, tiles)
-        load_page(2)
-        load_edit(3)
         load_w2(1)
-        load_page(3)
+        load_page(2)
         load_edit(4)
         load_wgs_dealt()
-        load_page(4)
         load_edit(5)
-        load_w3(0)
-        load_page(5)
         load_edit(6)
-        load_w3(1)
-        load_page(6)
         load_edit(7)
+        load_page(3)
         load_scales(nc.sync, w4_s, w4_scales)
         nc.sync.dma_start(
             out=w4_w[:].bitcast(I32),
             in_=w4_words.rearrange("a p c i -> p a (c i)").bitcast(I32),
         )
-        load_page(7)
+        load_page(4)
+        load_w3(0)
+        load_page(5)
+        load_w3(1)
+        load_page(6)
         load_audit(0)
+        load_page(7)
         load_audit(2)
 
         neg_temp = [held([P, PACK], F32, f"neg_temp{b}") for b in range(rp)]
@@ -217,20 +217,21 @@ def tile_list_repair_error_scores_kernel(
                     w1_q[a, u] = (codes[:, cols], scales[:, cols])
 
         def prepare_w1_dealt(a, slot):
+            scales = held([P, PASS], U8, f"w1_dealt_s{a}")
             grouped = ring.tile([P, PASS * PACK], BF16, name="grouped", align_bytes=64)
             nc.scalar.copy(
                 out=grouped[:].rearrange("p (i m j) -> p m j i", i=PACK, j=PACK),
                 in_=w1_raw[a, PACK][:].rearrange("p j (m i) -> p m j i", i=PACK),
             )
-            codes, scales = quantise(grouped[:], PASS, f"w1q_dealt{a}", slot)
+            nc.vector.quantize_mx(out=slot[:, a, :].bitcast(FP8X4), scales=scales[:], in_=grouped[:])
             for i in range(PACK):
-                w1_q[a, PACK + i] = (codes[:, i * P : (i + 1) * P], scales[:, i * P : (i + 1) * P])
+                w1_q[a, PACK + i] = (slot[:, a, i * P : (i + 1) * P], scales[:, i * P : (i + 1) * P])
 
         w2_wd = held([P, kp, 2 * PASS], U8, "w2_wd")
         w2_sd = {}
 
-        def deal_w2_scales(u):
-            w2_sd[1] = held([P, kp, PASS], U8, f"ready{u}")
+        def deal_w2_scales():
+            w2_sd[1] = held([P, kp, PASS], U8, "w2_sd")
             nc.vector.tensor_copy(
                 out=w2_sd[1][:].rearrange("p a (i m) -> p a i m", i=PACK),
                 in_=w2_s[:, :, PASS:].rearrange("p a (m i) -> p a i m", i=PACK),
@@ -268,15 +269,21 @@ def tile_list_repair_error_scores_kernel(
             banks[u] = (p1, p2)
 
         def gate(u):
-            gated[u] = ring.tile([P, S], F32, name="gated", bufs=2)
+            if PATHS[u] == "F":
+                first = ring.tile([P, S], F32, name="first", bufs=2)
+                nc.scalar.copy(out=first[:], in_=banks[u][0][:])
+                gated[u] = ring.tile([P, S], F32, name="gated_g", bufs=1)
+                nc.gpsimd.tensor_tensor(out=gated[u][:], in0=first[:], in1=edit_t[u][:], op=ALU.mult)
+                return
+            gated[u] = edit_t[u]
             nc.vector.tensor_tensor(out=gated[u][:], in0=banks[u][0][:], in1=edit_t[u][:], op=ALU.mult)
 
         def after_put(u):
             return held([P, S], U32, f"ready{u}")
 
         def weigh(u):
-            h = held([P, S], F32, f"ready{u}") if PATHS[u] == "V" else ring.tile([P, S], F32, name="h", bufs=2)
-            if PATHS[u] == "G":
+            h = held([P, S], F32, f"ready{u}") if PATHS[u] == "V" else ring.tile([P, S], F32, name="h", bufs=1)
+            if PATHS[u] in "GF":
                 second = ring.tile([P, S], F32, name="second", bufs=2)
                 nc.scalar.copy(out=second[:], in_=banks[u][1][:])
                 nc.gpsimd.tensor_tensor(out=h[:], in0=second[:], in1=gated[u][:], op=ALU.add)
@@ -284,6 +291,9 @@ def tile_list_repair_error_scores_kernel(
                 nc.vector.tensor_tensor(out=h[:], in0=banks[u][1][:], in1=gated[u][:], op=ALU.add)
             if PATHS[u] == "V":
                 ready[u] = h
+            elif PATHS[u] == "M":
+                ready[u] = held([P, S], F32, f"ready{u}")
+                nc.vector.tensor_tensor(out=ready[u][:], in0=h[:], in1=wgs_t[u], op=ALU.mult)
             else:
                 ready[u] = held([P, S], F32, f"ready{u}")
                 nc.gpsimd.tensor_tensor(out=ready[u][:], in0=h[:], in1=wgs_t[u], op=ALU.mult)
@@ -306,7 +316,7 @@ def tile_list_repair_error_scores_kernel(
             if u >= tiles - 2:
                 whole = held([P, PM], F32, "planes")
             else:
-                whole = ring.tile([P, PM], F32, name="x", bufs=2)
+                whole = held([P, PM], F32, "w2_w1")
             for part in range(parts):
                 x = whole[:, part * width : (part + 1) * width]
                 entries = idx3[:, part * width // 16 : (part + 1) * width // 16]
@@ -347,30 +357,32 @@ def tile_list_repair_error_scores_kernel(
         first_products(1)
         gate(0)
         weigh(0)
+        deal_w2_scales()
         for u in range(tiles):
             put(u)
-            if u + 1 < tiles:
-                gate(u + 1)
+            if u == 7:
+                z_q[0] = quantise(z_first[:], PM, "z0", after_put(u))
+            if u == 2:
+                dealt = held([P, kp, PASS], U32, f"ready{u}")
+                prepare_w1_dealt(0, dealt)
+                prepare_w1_dealt(1, dealt)
+                deal_w2_words()
+            if u in (5, 5 + 1):
+                prepare_w3(u - 5, after_put(u))
+            ahead = [[1], [2, 3], [4, 5, 6, 7]][u] if u < 3 else []
             row_max(u)
-            if u + 1 < tiles:
-                weigh(u + 1)
+            for v in ahead:
+                if v >= PACK:
+                    first_products(v)
+                gate(v)
+                weigh(v)
             if u == 0:
                 prepare_w1_plain(2, 4)
                 first_products(2)
                 first_products(3)
-            if u == 1:
-                deal_w2_scales(0)
-                prepare_w1_dealt(0, after_put(1))
-            if u == 2:
-                prepare_w1_dealt(1, after_put(2))
-                deal_w2_words()
-            if 2 <= u < tiles - 2:
-                first_products(u + 2)
-            if u in (4, 5):
-                prepare_w3(u - 4, after_put(u))
-            if u == 7:
-                z_q[0] = quantise(z_first[:], PM, "z0", after_put(u))
-            look(u)
+            if u >= 2:
+                for v in range(u + 1) if u == 2 else [u]:
+                    look(v)
             if u == PACK:
                 z_first = fetch_first_z()
 

@@ -1,6 +1,7 @@
 from contextlib import ExitStack
 
 import concourse.mybir as mybir
+from concourse.masks import make_identity
 
 K, T, S, T2, PM, H, N = 1024, 2048, 512, 1024, 512, 1024, 512
 FLOPS = 2 * 2 * K * H * S + 2 * 2 * H * N * PM
@@ -54,7 +55,7 @@ def tile_list_repair_error_scores_kernel(
         nc.vector.memset(w4_s[:].rearrange("p a t -> p (a t)").bitcast(I32), 0)
 
         def load_scales(queue, tile, src):
-            for q in range(4):
+            for q in (0, 2, 1, 3):
                 queue.dma_start(
                     out=tile[32 * q : 32 * q + 4].bitcast(I32),
                     in_=src[:, 4 * q : 4 * q + 4, :].rearrange("a r c -> r a c").bitcast(I32),
@@ -112,18 +113,33 @@ def tile_list_repair_error_scores_kernel(
                 in_=w3[b * PASS : (b + 1) * PASS, :].rearrange("(p j) c -> p j c", j=PACK),
             )
 
-        def load_audit(n0):
-            tile = held([P, 2, PM], F32, f"audit{n0}")
-            nc.sync.dma_start(out=tile[:], in_=audit[n0 * P : (n0 + 2) * P, :].rearrange("(n p) m -> p n m", p=P))
-            audit_t[n0], audit_t[n0 + 1] = tile[:, 0, :], tile[:, 1, :]
+        def load_audit():
+            tile = held([P, ntiles, PM], F32, "z_plain")
+            nc.sync.dma_start(out=tile[:], in_=audit.rearrange("(n p) m -> p n m", p=P))
+            for n in range(ntiles):
+                audit_t[n] = tile[:, n, :]
 
-        def load_per_row(vec, name):
-            first = held([P, PACK], F32, name + "0")
-            second = held([P, PACK], F32, name + "1")
-            with nc.allow_non_contiguous_dma(reason="one value a partition"):
-                nc.sync.dma_start(out=first[:], in_=vec[:PASS].rearrange("(u p) -> p u", p=P))
-            nc.sync.dma_start(out=second[:], in_=vec[PASS:].rearrange("(p i) -> p i", i=PACK))
-            return first, second
+        vec_rows = held([P, P], F32, "vec_rows")
+        identity = held([P, P], F32, "identity")
+        nc.gpsimd.memset(vec_rows[:], 0.0)
+        make_identity(nc, identity[:])
+        plain_cols = held([P, 2 * PACK], F32, "plain_cols")
+        temp_t = [plain_cols[:, :PACK], held([P, PACK], F32, "temp_dealt")]
+        gain_t = [plain_cols[:, PACK:], held([P, PACK], F32, "gain_dealt")]
+
+        def load_plain_rows():
+            for at, vec in ((0, temp), (PACK, gain)):
+                nc.sync.dma_start(out=vec_rows[at : at + PACK, :], in_=vec[:PASS].rearrange("(u p) -> u p", p=P))
+
+        def load_dealt_columns():
+            for tile, vec in ((temp_t[1], temp), (gain_t[1], gain)):
+                nc.sync.dma_start(out=tile[:], in_=vec[PASS:].rearrange("(p i) -> p i", i=PACK))
+
+        def load_dealt_edits():
+            tile = held([P, PACK, S], F32, "edit_dealt")
+            nc.sync.dma_start(out=tile[:], in_=edit[PASS:, :].rearrange("(p i) j -> p i j", i=PACK))
+            for i in range(PACK):
+                edit_t[PACK + i] = tile[:, i, :]
 
         wgs_plain = held([P, S], F32, "wgs_plain")
         w4_w = held([P, rp, N], U32, "w4_w")
@@ -131,48 +147,45 @@ def tile_list_repair_error_scores_kernel(
             wgs_t[u] = wgs_plain[:]
 
         nc.sync.dma_start(idx[:], offs)
-        load_w1(0, 1)
+        load_w1(0, 2)
         load_scales(nc.sync, tab_s, tab_scales)
         load_tab(0)
         load_tab(1)
         load_scales(nc.sync, w2_s, w2_scales)
         load_w2(0)
         load_edit(0)
-        load_w1(1, 2)
         nc.sync.dma_start(out=wgs_plain[:], in_=wgs)
         nc.sync.dma_start(idx2[:], offs2)
         load_page(0)
+        load_plain_rows()
         load_edit(1)
-        temp_t = load_per_row(temp, "temp")
         load_w1(2, 4)
         load_edit(2)
         load_edit(3)
         load_page(1)
         nc.sync.dma_start(idx3[:], offs3)
-        gain_t = load_per_row(gain, "gain")
+        load_dealt_columns()
         load_w1(PACK, tiles)
         load_w2(1)
         load_page(2)
-        load_edit(4)
+        load_dealt_edits()
         load_wgs_dealt()
-        load_edit(5)
-        load_edit(6)
-        load_edit(7)
         load_page(3)
+        load_w3(0)
+        load_page(4)
+        load_w3(1)
         load_scales(nc.sync, w4_s, w4_scales)
         nc.sync.dma_start(
             out=w4_w[:].bitcast(I32),
             in_=w4_words.rearrange("a p c i -> p a (c i)").bitcast(I32),
         )
-        load_page(4)
-        load_w3(0)
         load_page(5)
-        load_w3(1)
         load_page(6)
-        load_audit(0)
         load_page(7)
-        load_audit(2)
 
+        turned = psum.tile([P, P], F32, name="bank7")
+        nc.tensor.transpose(turned[:], vec_rows[:], identity[:])
+        nc.scalar.copy(out=plain_cols[:], in_=turned[:, : 2 * PACK])
         neg_temp = [held([P, PACK], F32, f"neg_temp{b}") for b in range(rp)]
         for b in range(rp):
             nc.scalar.mul(neg_temp[b][:], temp_t[b][:], -1.0)
@@ -275,7 +288,7 @@ def tile_list_repair_error_scores_kernel(
                 gated[u] = ring.tile([P, S], F32, name="gated_g", bufs=1)
                 nc.gpsimd.tensor_tensor(out=gated[u][:], in0=first[:], in1=edit_t[u][:], op=ALU.mult)
                 return
-            gated[u] = edit_t[u]
+            gated[u] = held([P, S], F32, f"ready{u - 3}") if u >= tiles - 2 else edit_t[u]
             nc.vector.tensor_tensor(out=gated[u][:], in0=banks[u][0][:], in1=edit_t[u][:], op=ALU.mult)
 
         def after_put(u):
@@ -335,25 +348,28 @@ def tile_list_repair_error_scores_kernel(
                     )
 
         def prepare_w3(b, slot):
+            scales = held([P, N], U8, f"w3_s{b}")
             grouped = ring.tile([P, N * PACK], BF16, name="grouped", align_bytes=64)
             interleave(grouped[:], w3_raw[b][:])
-            w3_q[b] = quantise(grouped[:], N, f"w3q{b}", slot)
+            nc.vector.quantize_mx(out=slot[:, b, :].bitcast(FP8X4), scales=scales[:], in_=grouped[:])
+            w3_q[b] = (slot[:, b, :], scales)
 
         def fetch_first_z():
-            nc.sync.dma_start(out=out.rearrange("(u p) m -> p u m", p=P), in_=z_plain[:])
+            parked = out.rearrange("(u p) m -> p u m", p=P)
+            for u0, u1 in ((0, PACK - 1), (PACK - 1, PACK)):
+                nc.sync.dma_start(out=parked[:, u0:u1, :], in_=z_plain[:, u0:u1, :])
             planes = held([P, PACK, PM], F32, "planes")
             nc.sync.dma_start(out=planes[:], in_=out.rearrange("(p i) m -> p i m", i=PACK))
             grouped = held([P, PM * PACK], BF16, "z_first")
             interleave(grouped[:], planes[:])
             return grouped
 
-        prepare_w1_plain(0, 1)
+        prepare_w1_plain(0, 2)
         gather_scales(0)
         gather_scales(1)
         gather_words(0)
         gather_words(1)
         first_products(0)
-        prepare_w1_plain(1, 2)
         first_products(1)
         gate(0)
         weigh(0)
@@ -367,9 +383,11 @@ def tile_list_repair_error_scores_kernel(
                 prepare_w1_dealt(0, dealt)
                 prepare_w1_dealt(1, dealt)
                 deal_w2_words()
-            if u in (5, 5 + 1):
-                prepare_w3(u - 5, after_put(u))
-            ahead = [[1], [2, 3], [4, 5, 6, 7]][u] if u < 3 else []
+            if u == 6:
+                both = held([P, rp, N], U32, f"ready{u}")
+                prepare_w3(0, both)
+                prepare_w3(1, both)
+            ahead = [[1], [2, 3], [4, 5], [6], [7]][u] if u < 5 else []
             row_max(u)
             for v in ahead:
                 if v >= PACK:
@@ -385,6 +403,7 @@ def tile_list_repair_error_scores_kernel(
                     look(v)
             if u == PACK:
                 z_first = fetch_first_z()
+                load_audit()
 
         acc = [
             (psum.tile([P, PM], F32, name=f"bank{2 * n}"), psum.tile([P, PM], F32, name=f"bank{2 * n + 1}"))

@@ -20,8 +20,18 @@ ACT = mybir.ActivationFunctionType
 P = 128
 PACK = 4
 PASS = P * PACK
-PATHS = "VVMGGGGG"
-TAIL_G = 2
+K_PASSES = K // PASS
+R_PASSES = H // PASS
+TILES = H // P
+PLAIN = PACK
+LAST = TILES - 1
+OUT_TILES = N // P
+QUADRANTS = (0, 2, 1, 3)
+
+FUSED = 2
+POOL_SUM = 3
+POOL_EDIT = 6
+POOL_OUT = 2
 
 
 def tile_list_repair_error_scores_kernel(
@@ -29,10 +39,6 @@ def tile_list_repair_error_scores_kernel(
     offs2, offs3, temp, gain, w3, w4_words, w4_scales, audit, out,
 ):
     nc = tc.nc
-    kp = K // PASS
-    rp = H // PASS
-    tiles = H // P
-    ntiles = N // P
 
     with ExitStack() as ctx:
         lists = ctx.enter_context(tc.tile_pool(name="lists", bufs=1))
@@ -40,49 +46,46 @@ def tile_list_repair_error_scores_kernel(
         ring = ctx.enter_context(tc.tile_pool(name="ring", bufs=3))
         psum = ctx.enter_context(tc.psum_pool(name="psum", bufs=1))
 
-        def held(shape, dtype, name):
-            return keep.tile(shape, dtype, name=name, align_bytes=64)
+        def held(shape, dtype, name, slot=None):
+            return keep.tile(shape, dtype, name=name, tag=slot or name, align_bytes=64)
 
         idx = lists.tile([P, S // 16], U16, name="idx")
         idx2 = lists.tile([P, S // 16], U16, name="idx2")
         idx3 = lists.tile([P, PM // 16], U16, name="idx3")
 
-        tab_s = held([P, kp, T], U8, "tab_s")
-        w2_s = held([P, kp, H], U8, "w2_s")
-        w4_s = held([P, rp, N], U8, "w4_s")
+        tab_s = held([P, K_PASSES, T], U8, "tab_s")
+        w2_s = held([P, K_PASSES, H], U8, "w2_s")
+        w4_s = held([P, R_PASSES, N], U8, "w4_s")
         nc.vector.memset(tab_s[:].rearrange("p a t -> p (a t)").bitcast(I32), 0)
         nc.gpsimd.memset(w2_s[:].rearrange("p a t -> p (a t)").bitcast(I32), 0)
         nc.vector.memset(w4_s[:].rearrange("p a t -> p (a t)").bitcast(I32), 0)
 
-        def load_scales(queue, tile, src):
-            for q in (0, 2, 1, 3):
-                queue.dma_start(
+        w1_raw, w2_w, tab_w, w3_raw, edit_t, page, wgs_t, audit_t = {}, {}, {}, {}, {}, {}, {}, {}
+
+        def load_scales(tile, src):
+            for q in QUADRANTS:
+                nc.sync.dma_start(
                     out=tile[32 * q : 32 * q + 4].bitcast(I32),
                     in_=src[:, 4 * q : 4 * q + 4, :].rearrange("a r c -> r a c").bitcast(I32),
                 )
 
-        def rows_of(src, u):
-            if u < PACK:
-                return src[u * P : (u + 1) * P, :]
-            return src[PASS:, :].rearrange("(p i) c -> i p c", i=PACK)[u - PACK]
+        def load_w1_rows(raw, a, u0, u1):
+            w1_raw[a, u0] = raw
+            rows = w1[a * PASS : (a + 1) * PASS, u0 * P : u1 * P]
+            nc.sync.dma_start(out=raw[:], in_=rows.rearrange("(p j) c -> p j c", j=PACK))
 
-        w1_raw, w2_w, tab_w, w3_raw, edit_t, page, wgs_t, audit_t = {}, {}, {}, {}, {}, {}, {}, {}
+        def load_w1_plain(u0, u1):
+            for a in range(K_PASSES):
+                load_w1_rows(held([P, PACK, (u1 - u0) * P], F32, f"w1_raw{a}{u0}"), a, u0, u1)
 
-        def load_w1(u0, u1):
-            width = (u1 - u0) * P
-            for a in range(kp):
-                if width == PASS:
-                    raw = ring.tile([P, PACK, PASS], F32, name="raw", bufs=3)
-                else:
-                    raw = held([P, PACK, width], F32, f"w1_raw{a}{u0}")
-                w1_raw[a, u0] = raw
-                rows = w1[a * PASS : (a + 1) * PASS, u0 * P : u1 * P]
-                nc.sync.dma_start(out=raw[:], in_=rows.rearrange("(p j) c -> p j c", j=PACK))
+        def load_w1_dealt():
+            load_w1_rows(ring.tile([P, PACK, PASS], F32, name="raw", bufs=2), 0, PLAIN, TILES)
+            load_w1_rows(held([P, PACK, PASS], F32, "w1_raw_last"), 1, PLAIN, TILES)
 
-        def load_w2(b):
-            w2_w[b] = held([P, kp, 2 * PASS], U8, f"w2_w{b}")
-            src = w2_words[:, :, 2 * b * PASS : 2 * (b + 1) * PASS]
-            nc.sync.dma_start(out=w2_w[b][:].bitcast(I32), in_=src.rearrange("a p c -> p a c").bitcast(I32))
+        def load_w2(half):
+            w2_w[half] = held([P, K_PASSES, 2 * PASS], U8, f"w2_w{half}")
+            src = w2_words[:, :, 2 * half * PASS : 2 * (half + 1) * PASS]
+            nc.sync.dma_start(out=w2_w[half][:].bitcast(I32), in_=src.rearrange("a p c -> p a c").bitcast(I32))
 
         def load_tab(a):
             tab_w[a] = held([P, T], U32, f"tab_w{a}")
@@ -91,109 +94,113 @@ def tile_list_repair_error_scores_kernel(
                 in_=tab_words[a].rearrange("p t i -> p (t i)").bitcast(I32),
             )
 
-        def load_edit(u):
+        def load_edit_plain(u):
             edit_t[u] = held([P, S], F32, f"edit{u}")
-            nc.sync.dma_start(out=edit_t[u][:], in_=rows_of(edit, u))
+            nc.sync.dma_start(out=edit_t[u][:], in_=edit[u * P : (u + 1) * P, :])
+
+        def load_edit_dealt():
+            tile = held([P, PACK, S], F32, "edit_dealt")
+            nc.sync.dma_start(out=tile[:], in_=edit[PASS:, :].rearrange("(p i) j -> p i j", i=PACK))
+            for i in range(PACK):
+                edit_t[PLAIN + i] = tile[:, i, :]
 
         def load_page(u):
             page[u] = held([P, T2], F32, f"page{u}")
-            nc.sync.dma_start(out=page[u][:], in_=rows_of(page0, u))
+            if u < PLAIN:
+                rows = page0[u * P : (u + 1) * P, :]
+            else:
+                rows = page0[PASS:, :].rearrange("(p i) c -> i p c", i=PACK)[u - PLAIN]
+            nc.sync.dma_start(out=page[u][:], in_=rows)
 
         def load_wgs_dealt():
             tile = held([P, PACK, S], F32, "wgs_dealt")
-            for q in (0, 2, 1, 3):
+            for q in QUADRANTS:
                 nc.sync.dma_start(out=tile[32 * q : 32 * q + 32], in_=wgs.rearrange("(q i) j -> q i j", i=PACK))
             for i in range(PACK):
-                wgs_t[PACK + i] = tile[:, i, :]
+                wgs_t[PLAIN + i] = tile[:, i, :]
 
         def load_w3(b):
-            w3_raw[b] = ring.tile([P, PACK, N], F32, name="raw", bufs=3)
+            w3_raw[b] = ring.tile([P, PACK, N], F32, name="raw", bufs=2)
             nc.sync.dma_start(
                 out=w3_raw[b][:],
                 in_=w3[b * PASS : (b + 1) * PASS, :].rearrange("(p j) c -> p j c", j=PACK),
             )
 
         def load_audit():
-            tile = held([P, ntiles, PM], F32, "z_plain")
+            tile = held([P, OUT_TILES, PM], F32, "audit", slot="z_plain")
             nc.sync.dma_start(out=tile[:], in_=audit.rearrange("(n p) m -> p n m", p=P))
-            for n in range(ntiles):
+            for n in range(OUT_TILES):
                 audit_t[n] = tile[:, n, :]
 
         vec_rows = held([P, P], F32, "vec_rows")
         identity = held([P, P], F32, "identity")
         nc.gpsimd.memset(vec_rows[:], 0.0)
         make_identity(nc, identity[:])
-        plain_cols = held([P, 2 * PACK], F32, "plain_cols")
-        temp_t = [plain_cols[:, :PACK], held([P, PACK], F32, "temp_dealt")]
-        gain_t = [plain_cols[:, PACK:], held([P, PACK], F32, "gain_dealt")]
+        plain_cols = held([P, 2 * PLAIN], F32, "plain_cols")
+        temp_t = [plain_cols[:, :PLAIN], held([P, PACK], F32, "temp_dealt")]
+        gain_t = [plain_cols[:, PLAIN:], held([P, PACK], F32, "gain_dealt")]
 
-        def load_plain_rows():
-            for at, vec in ((0, temp), (PACK, gain)):
-                nc.sync.dma_start(out=vec_rows[at : at + PACK, :], in_=vec[:PASS].rearrange("(u p) -> u p", p=P))
+        def load_vectors_plain():
+            for at, vec in ((0, temp), (PLAIN, gain)):
+                nc.sync.dma_start(out=vec_rows[at : at + PLAIN, :], in_=vec[:PASS].rearrange("(u p) -> u p", p=P))
 
-        def load_dealt_columns():
+        def load_vectors_dealt():
             for tile, vec in ((temp_t[1], temp), (gain_t[1], gain)):
                 nc.sync.dma_start(out=tile[:], in_=vec[PASS:].rearrange("(p i) -> p i", i=PACK))
 
-        def load_dealt_edits():
-            tile = held([P, PACK, S], F32, "edit_dealt")
-            nc.sync.dma_start(out=tile[:], in_=edit[PASS:, :].rearrange("(p i) j -> p i j", i=PACK))
-            for i in range(PACK):
-                edit_t[PACK + i] = tile[:, i, :]
-
         wgs_plain = held([P, S], F32, "wgs_plain")
-        w4_w = held([P, rp, N], U32, "w4_w")
-        for u in range(PACK):
+        w4_w = held([P, R_PASSES, N], U32, "w4_w")
+        for u in range(PLAIN):
             wgs_t[u] = wgs_plain[:]
 
         nc.sync.dma_start(idx[:], offs)
-        load_w1(0, 2)
-        load_scales(nc.sync, tab_s, tab_scales)
+        load_w1_plain(0, 2)
+        load_scales(tab_s, tab_scales)
         load_tab(0)
         load_tab(1)
-        load_scales(nc.sync, w2_s, w2_scales)
+        load_scales(w2_s, w2_scales)
         load_w2(0)
-        load_edit(0)
+        load_edit_plain(0)
         nc.sync.dma_start(out=wgs_plain[:], in_=wgs)
         nc.sync.dma_start(idx2[:], offs2)
         load_page(0)
-        load_plain_rows()
-        load_edit(1)
-        load_w1(2, 4)
-        load_edit(2)
-        load_edit(3)
-        load_page(1)
+        load_vectors_plain()
+        load_edit_plain(1)
         nc.sync.dma_start(idx3[:], offs3)
-        load_dealt_columns()
-        load_w1(PACK, tiles)
+        load_w1_plain(2, PLAIN)
+        load_edit_plain(2)
+        load_edit_plain(3)
+        load_page(1)
         load_w2(1)
+        load_w1_dealt()
         load_page(2)
-        load_dealt_edits()
-        load_wgs_dealt()
-        load_page(3)
+        load_edit_dealt()
         load_w3(0)
+        load_page(3)
+        load_wgs_dealt()
+        load_vectors_dealt()
         load_page(4)
         load_w3(1)
-        load_scales(nc.sync, w4_s, w4_scales)
+        load_page(5)
+        load_scales(w4_s, w4_scales)
         nc.sync.dma_start(
             out=w4_w[:].bitcast(I32),
             in_=w4_words.rearrange("a p c i -> p a (c i)").bitcast(I32),
         )
-        load_page(5)
         load_page(6)
-        load_page(7)
+        load_page(LAST)
 
         turned = psum.tile([P, P], F32, name="bank7")
         nc.tensor.transpose(turned[:], vec_rows[:], identity[:])
-        nc.scalar.copy(out=plain_cols[:], in_=turned[:, : 2 * PACK])
-        neg_temp = [held([P, PACK], F32, f"neg_temp{b}") for b in range(rp)]
-        for b in range(rp):
-            nc.scalar.mul(neg_temp[b][:], temp_t[b][:], -1.0)
+        nc.scalar.copy(out=plain_cols[:], in_=turned[:, : 2 * PLAIN])
+        neg_temp = [held([P, PACK], F32, f"neg_temp{half}") for half in range(R_PASSES)]
+        for half in range(R_PASSES):
+            nc.scalar.mul(neg_temp[half][:], temp_t[half][:], -1.0)
 
-        def column(pair, u):
-            return pair[u // PACK][:, u % PACK : u % PACK + 1]
+        def column(halves, u):
+            return halves[u // PACK][:, u % PACK : u % PACK + 1]
 
-        v_s, v_w = {}, {}
+        v_s, v_w, w1_q, w3_grouped, w3_q, z_q = {}, {}, {}, {}, {}, {}
 
         def gather_scales(a):
             v_s[a] = held([P, S], U8, f"v_s{a}")
@@ -203,239 +210,255 @@ def tile_list_repair_error_scores_kernel(
             v_w[a] = held([P, S], U32, f"v_w{a}")
             nc.vector.tensor_copy(v_w[a][:], tab_w[a][:].indirect(idx[:]))
 
-        def quantise(grouped, width, name, codes=None):
-            if codes is None:
-                codes = held([P, width], U32, name + "_c")
-            scales = held([P, width], U8, name + "_s")
-            nc.vector.quantize_mx(out=codes[:].bitcast(FP8X4), scales=scales[:], in_=grouped)
+        def quantise(codes, grouped, name):
+            scales = held([P, codes.shape[1]], U8, name)
+            nc.vector.quantize_mx(out=codes.bitcast(FP8X4), scales=scales[:], in_=grouped)
             return codes, scales
 
-        def interleave(dst, src):
+        def interleave(grouped, rows):
             nc.scalar.copy(
-                out=dst.rearrange("p (c e j) -> p c j e", e=4, j=PACK),
-                in_=src.rearrange("p j (c e) -> p c j e", e=4),
+                out=grouped.rearrange("p (c e j) -> p c j e", e=4, j=PACK),
+                in_=rows.rearrange("p j (c e) -> p c j e", e=4),
             )
-
-        w1_q = {}
 
         def prepare_w1_plain(u0, u1):
             width = (u1 - u0) * P
-            grouped = ring.tile([P, kp, width * PACK], BF16, name="grouped", align_bytes=64)
-            for a in range(kp):
+            grouped = ring.tile([P, K_PASSES, width * PACK], BF16, name="grouped", align_bytes=64)
+            for a in range(K_PASSES):
                 interleave(grouped[:, a, :], w1_raw[a, u0][:])
-            codes, scales = quantise(grouped[:].rearrange("p a c -> p (a c)"), kp * width, f"w1q{u0}")
-            for a in range(kp):
+            codes = held([P, K_PASSES * width], U32, f"w1_codes{u0}")
+            codes, scales = quantise(codes[:], grouped[:].rearrange("p a c -> p (a c)"), f"w1_scales{u0}")
+            for a in range(K_PASSES):
                 for u in range(u0, u1):
                     cols = slice(a * width + (u - u0) * P, a * width + (u - u0 + 1) * P)
                     w1_q[a, u] = (codes[:, cols], scales[:, cols])
 
-        def prepare_w1_dealt(a, slot):
-            scales = held([P, PASS], U8, f"w1_dealt_s{a}")
-            grouped = ring.tile([P, PASS * PACK], BF16, name="grouped", align_bytes=64)
+        def prepare_w1_dealt(a, grouped, codes):
             nc.scalar.copy(
                 out=grouped[:].rearrange("p (i m j) -> p m j i", i=PACK, j=PACK),
-                in_=w1_raw[a, PACK][:].rearrange("p j (m i) -> p m j i", i=PACK),
+                in_=w1_raw[a, PLAIN][:].rearrange("p j (m i) -> p m j i", i=PACK),
             )
-            nc.vector.quantize_mx(out=slot[:, a, :].bitcast(FP8X4), scales=scales[:], in_=grouped[:])
+            codes, scales = quantise(codes, grouped[:], f"w1_scales_dealt{a}")
             for i in range(PACK):
-                w1_q[a, PACK + i] = (slot[:, a, i * P : (i + 1) * P], scales[:, i * P : (i + 1) * P])
+                w1_q[a, PLAIN + i] = (codes[:, i * P : (i + 1) * P], scales[:, i * P : (i + 1) * P])
 
-        w2_wd = held([P, kp, 2 * PASS], U8, "w2_wd")
-        w2_sd = {}
+        w2_w_dealt = held([P, K_PASSES, 2 * PASS], U8, "w2_w_dealt")
+        w2_s_dealt = held([P, K_PASSES, PASS], U8, "w2_s_dealt")
 
         def deal_w2_scales():
-            w2_sd[1] = held([P, kp, PASS], U8, "w2_sd")
             nc.vector.tensor_copy(
-                out=w2_sd[1][:].rearrange("p a (i m) -> p a i m", i=PACK),
+                out=w2_s_dealt[:].rearrange("p a (i m) -> p a i m", i=PACK),
                 in_=w2_s[:, :, PASS:].rearrange("p a (m i) -> p a i m", i=PACK),
             )
 
         def deal_w2_words():
             nc.scalar.copy(
-                out=w2_wd[:].bitcast(U16).rearrange("p a (i m) -> p a i m", i=PACK),
+                out=w2_w_dealt[:].bitcast(U16).rearrange("p a (i m) -> p a i m", i=PACK),
                 in_=w2_w[1][:].bitcast(U16).rearrange("p a (m i) -> p a i m", i=PACK),
             )
 
-        bias = held([P, tiles], F32, "bias")
-        scaled = held([P, T2], F32, "scaled")
-        z_plain = held([P, PACK, PM], F32, "z_plain")
-        z_last = held([P, PM, PACK], BF16, "z_last")
-        banks, z_q, w3_q, gated, ready = {}, {}, {}, {}, {}
+        def round_w3(b):
+            w3_grouped[b] = ring.tile([P, N * PACK], BF16, name="grouped", align_bytes=64)
+            interleave(w3_grouped[b][:], w3_raw[b][:])
+
+        bias = held([P, TILES], F32, "bias")
+        z_plain = held([P, PLAIN, PM], F32, "z_plain")
+        z_dealt = held([P, PM, PACK], BF16, "z_dealt")
+        banks, edited, to_put = {}, {}, {}
 
         def first_products(u):
             i = u % PACK
-            words, bytes_ = (w2_w[0], w2_s) if u < PACK else (w2_wd, w2_sd[1])
-            p1 = psum.tile([P, S], F32, name=f"bank{2 * i}")
-            p2 = psum.tile([P, S], F32, name=f"bank{2 * i + 1}")
-            for a in range(kp):
+            words, scale_bytes = (w2_w[0], w2_s) if u < PLAIN else (w2_w_dealt, w2_s_dealt)
+            by_w1 = psum.tile([P, S], F32, name=f"bank{2 * i}")
+            by_w2 = psum.tile([P, S], F32, name=f"bank{2 * i + 1}")
+            for a in range(K_PASSES):
                 codes, scales = w1_q[a, u]
                 nc.tensor.matmul_mx(
-                    out=p1[:], lhsT=codes.bitcast(FP8X4), lhsT_scale=scales,
-                    rhs=v_w[a][:].bitcast(FP8X4), rhs_scale=v_s[a][:], start=(a == 0), stop=(a == kp - 1),
+                    out=by_w1[:], lhsT=codes.bitcast(FP8X4), lhsT_scale=scales,
+                    rhs=v_w[a][:].bitcast(FP8X4), rhs_scale=v_s[a][:],
+                    start=(a == 0), stop=(a == K_PASSES - 1),
                 )
-            for a in range(kp):
+            for a in range(K_PASSES):
                 nc.tensor.matmul_mx(
-                    out=p2[:], lhsT=words[:, a, 2 * i * P : 2 * (i + 1) * P].bitcast(FP4X4),
-                    lhsT_scale=bytes_[:, a, i * P : (i + 1) * P],
-                    rhs=v_w[a][:].bitcast(FP8X4), rhs_scale=v_s[a][:], start=(a == 0), stop=(a == kp - 1),
+                    out=by_w2[:], lhsT=words[:, a, 2 * i * P : 2 * (i + 1) * P].bitcast(FP4X4),
+                    lhsT_scale=scale_bytes[:, a, i * P : (i + 1) * P],
+                    rhs=v_w[a][:].bitcast(FP8X4), rhs_scale=v_s[a][:],
+                    start=(a == 0), stop=(a == K_PASSES - 1),
                 )
-            banks[u] = (p1, p2)
+            banks[u] = (by_w1, by_w2)
 
-        def gate(u):
-            if PATHS[u] == "F":
-                first = ring.tile([P, S], F32, name="first", bufs=2)
-                nc.scalar.copy(out=first[:], in_=banks[u][0][:])
-                gated[u] = ring.tile([P, S], F32, name="gated_g", bufs=1)
-                nc.gpsimd.tensor_tensor(out=gated[u][:], in0=first[:], in1=edit_t[u][:], op=ALU.mult)
-                return
-            gated[u] = held([P, S], F32, f"ready{u - 3}") if u >= tiles - 2 else edit_t[u]
-            nc.vector.tensor_tensor(out=gated[u][:], in0=banks[u][0][:], in1=edit_t[u][:], op=ALU.mult)
+        def times_edit(u):
+            if u >= POOL_EDIT:
+                by_w1 = held([P, S], F32, f"by_w1_{u}", slot="w2_w0" if u == LAST else None)
+                nc.scalar.copy(out=by_w1[:], in_=banks[u][0][:])
+                edited[u] = held([P, S], F32, f"edited{u}", slot="h")
+                nc.gpsimd.tensor_tensor(out=edited[u][:], in0=by_w1[:], in1=edit_t[u][:], op=ALU.mult)
+            else:
+                edited[u] = held([P, S], F32, f"edited{u}", slot=f"to_put{u - 2}") if u > PLAIN else edit_t[u]
+                nc.vector.tensor_tensor(out=edited[u][:], in0=banks[u][0][:], in1=edit_t[u][:], op=ALU.mult)
 
-        def after_put(u):
-            return held([P, S], U32, f"ready{u}")
+        def sum_products(u):
+            if u >= POOL_EDIT:
+                h = edited[u]
+            else:
+                h = held([P, S], F32, f"h{u}", slot=f"to_put{u}" if u < FUSED else "h")
+            if u >= POOL_SUM:
+                spent_w1 = f"w1_raw{u % 2}{2 * ((u - PLAIN) // 2)}"
+                by_w2 = held([P, S], F32, f"by_w2_{u}", slot=spent_w1 if u >= PLAIN else None)
+                nc.scalar.copy(out=by_w2[:], in_=banks[u][1][:])
+                nc.gpsimd.tensor_tensor(out=h[:], in0=by_w2[:], in1=edited[u][:], op=ALU.add)
+            else:
+                nc.vector.tensor_tensor(out=h[:], in0=banks[u][1][:], in1=edited[u][:], op=ALU.add)
+            return h
 
         def weigh(u):
-            h = held([P, S], F32, f"ready{u}") if PATHS[u] == "V" else ring.tile([P, S], F32, name="h", bufs=1)
-            if PATHS[u] in "GF":
-                second = ring.tile([P, S], F32, name="second", bufs=2)
-                nc.scalar.copy(out=second[:], in_=banks[u][1][:])
-                nc.gpsimd.tensor_tensor(out=h[:], in0=second[:], in1=gated[u][:], op=ALU.add)
+            h = sum_products(u)
+            if u < FUSED:
+                to_put[u] = h
             else:
-                nc.vector.tensor_tensor(out=h[:], in0=banks[u][1][:], in1=gated[u][:], op=ALU.add)
-            if PATHS[u] == "V":
-                ready[u] = h
-            elif PATHS[u] == "M":
-                ready[u] = held([P, S], F32, f"ready{u}")
-                nc.vector.tensor_tensor(out=ready[u][:], in0=h[:], in1=wgs_t[u], op=ALU.mult)
-            else:
-                ready[u] = held([P, S], F32, f"ready{u}")
-                nc.gpsimd.tensor_tensor(out=ready[u][:], in0=h[:], in1=wgs_t[u], op=ALU.mult)
+                to_put[u] = held([P, S], F32, f"to_put{u}")
+                engine = nc.gpsimd if u >= POOL_SUM else nc.vector
+                engine.tensor_tensor(out=to_put[u][:], in0=h[:], in1=wgs_t[u], op=ALU.mult)
 
         def put(u):
-            if PATHS[u] == "V":
-                nc.vector.tensor_tensor(page[u][:].indirect(idx2[:]), ready[u][:], wgs_t[u], ALU.mult)
+            if u < FUSED:
+                nc.vector.tensor_tensor(page[u][:].indirect(idx2[:]), to_put[u][:], wgs_t[u], ALU.mult)
             else:
-                nc.vector.tensor_copy(page[u][:].indirect(idx2[:]), ready[u][:])
+                nc.vector.tensor_copy(page[u][:].indirect(idx2[:]), to_put[u][:])
 
-        def row_max(u):
+        def row_bias(u):
+            scratch = held([P, T2], F32, f"scratch{u}", slot="scratch" if u < FUSED else "grouped_last")
             nc.vector.tensor_scalar(
-                out=scaled[:], in0=page[u][:], scalar1=column(neg_temp, u), scalar2=None,
+                out=scratch[:], in0=page[u][:], scalar1=column(neg_temp, u), scalar2=None,
                 op0=ALU.mult, op1=ALU.min, accum_out=bias[:, u : u + 1],
             )
 
         def look(u):
-            parts = 2 if u == tiles - 1 else 1
+            slot = "w1_raw12" if u == 0 else "z_back" if u >= LAST - 1 else "w1_raw_last"
+            x = held([P, PM], F32, f"x{u}", slot=slot)
+            parts = 2 if u == LAST else 1
             width = PM // parts
-            if u >= tiles - 2:
-                whole = held([P, PM], F32, "planes")
-            else:
-                whole = held([P, PM], F32, "w2_w1")
             for part in range(parts):
-                x = whole[:, part * width : (part + 1) * width]
+                cols = slice(part * width, (part + 1) * width)
                 entries = idx3[:, part * width // 16 : (part + 1) * width // 16]
                 nc.scalar.activation(
-                    out=x, in_=page[u][:].indirect(entries), func=ACT.Exp,
+                    out=x[:, cols], in_=page[u][:].indirect(entries), func=ACT.Exp,
                     bias=bias[:, u : u + 1], scale=column(temp_t, u),
                 )
-                if u < PACK:
-                    nc.scalar.activation(out=z_plain[:, u, :], in_=x, func=ACT.Copy, scale=column(gain_t, u))
-                elif parts == 1:
-                    nc.scalar.activation(out=z_last[:, :, u - PACK], in_=x, func=ACT.Copy, scale=column(gain_t, u))
+                if u < PLAIN:
+                    nc.scalar.activation(out=z_plain[:, u, :], in_=x[:, cols], func=ACT.Copy, scale=column(gain_t, u))
+                elif u < LAST:
+                    nc.scalar.activation(
+                        out=z_dealt[:, cols, u - PLAIN], in_=x[:, cols], func=ACT.Copy, scale=column(gain_t, u),
+                    )
                 else:
                     nc.vector.tensor_scalar(
-                        out=z_last[:, part * width : (part + 1) * width, u - PACK], in0=x,
+                        out=z_dealt[:, cols, u - PLAIN], in0=x[:, cols],
                         scalar1=column(gain_t, u), scalar2=None, op0=ALU.mult,
                     )
 
-        def prepare_w3(b, slot):
-            scales = held([P, N], U8, f"w3_s{b}")
-            grouped = ring.tile([P, N * PACK], BF16, name="grouped", align_bytes=64)
-            interleave(grouped[:], w3_raw[b][:])
-            nc.vector.quantize_mx(out=slot[:, b, :].bitcast(FP8X4), scales=scales[:], in_=grouped[:])
-            w3_q[b] = (slot[:, b, :], scales)
-
-        def fetch_first_z():
+        def regroup_plain_z():
             parked = out.rearrange("(u p) m -> p u m", p=P)
-            for u0, u1 in ((0, PACK - 1), (PACK - 1, PACK)):
+            for u0, u1 in ((0, PLAIN - 1), (PLAIN - 1, PLAIN)):
                 nc.sync.dma_start(out=parked[:, u0:u1, :], in_=z_plain[:, u0:u1, :])
-            planes = held([P, PACK, PM], F32, "planes")
-            nc.sync.dma_start(out=planes[:], in_=out.rearrange("(p i) m -> p i m", i=PACK))
-            grouped = held([P, PM * PACK], BF16, "z_first")
-            interleave(grouped[:], planes[:])
+            z_back = held([P, PACK, PM], F32, "z_back")
+            nc.sync.dma_start(out=z_back[:], in_=out.rearrange("(p i) m -> p i m", i=PACK))
+            grouped = held([P, PM * PACK], BF16, "z_grouped")
+            interleave(grouped[:], z_back[:])
             return grouped
 
+        def prepare_tile(u):
+            if u >= PLAIN:
+                first_products(u)
+            times_edit(u)
+            weigh(u)
+
         prepare_w1_plain(0, 2)
-        gather_scales(0)
-        gather_scales(1)
-        gather_words(0)
-        gather_words(1)
+        for a in range(K_PASSES):
+            gather_scales(a)
+        for a in range(K_PASSES):
+            gather_words(a)
         first_products(0)
         first_products(1)
-        gate(0)
-        weigh(0)
+        prepare_tile(0)
         deal_w2_scales()
-        for u in range(tiles):
+
+        put(0)
+        row_bias(0)
+        prepare_tile(1)
+        prepare_w1_plain(2, PLAIN)
+        first_products(2)
+        first_products(3)
+        look(0)
+
+        put(1)
+        row_bias(1)
+        prepare_tile(2)
+        prepare_tile(3)
+
+        put(2)
+        w1_codes = held([P, K_PASSES, PASS], U32, "w1_codes_dealt", slot="to_put2")
+        grouped_first = ring.tile([P, PASS * PACK], BF16, name="grouped", align_bytes=64)
+        prepare_w1_dealt(0, grouped_first, w1_codes[:, 0, :])
+        prepare_w1_dealt(1, held([P, PASS * PACK], BF16, "grouped_last"), w1_codes[:, 1, :])
+        deal_w2_words()
+        row_bias(2)
+        prepare_tile(PLAIN)
+        look(1)
+        look(2)
+        round_w3(0)
+
+        for u in range(3, TILES):
             put(u)
-            if u == 7:
-                z_q[0] = quantise(z_first[:], PM, "z0", after_put(u))
-            if u == 2:
-                dealt = held([P, kp, PASS], U32, f"ready{u}")
-                prepare_w1_dealt(0, dealt)
-                prepare_w1_dealt(1, dealt)
-                deal_w2_words()
-            if u == 6:
-                both = held([P, rp, N], U32, f"ready{u}")
-                prepare_w3(0, both)
-                prepare_w3(1, both)
-            ahead = [[1], [2, 3], [4, 5], [6], [7]][u] if u < 5 else []
-            row_max(u)
-            for v in ahead:
-                if v >= PACK:
-                    first_products(v)
-                gate(v)
-                weigh(v)
-            if u == 0:
-                prepare_w1_plain(2, 4)
-                first_products(2)
-                first_products(3)
-            if u >= 2:
-                for v in range(u + 1) if u == 2 else [u]:
-                    look(v)
-            if u == PACK:
-                z_first = fetch_first_z()
+            if u == LAST:
+                z_codes = held([P, PM], U32, "z_codes0", slot=f"to_put{u}")
+                z_q[0] = quantise(z_codes[:], z_grouped[:], "z_scales0")
+            if u == LAST - 1:
+                w3_codes = held([P, R_PASSES, N], U32, "w3_codes", slot=f"to_put{u}")
+                for b in range(R_PASSES):
+                    w3_q[b] = quantise(w3_codes[:, b, :], w3_grouped[b][:], f"w3_scales{b}")
+            if u + 2 < TILES:
+                prepare_tile(u + 2)
+            row_bias(u)
+            look(u)
+            if u == PLAIN - 1:
+                round_w3(1)
+            if u == PLAIN:
+                z_grouped = regroup_plain_z()
                 load_audit()
 
         acc = [
             (psum.tile([P, PM], F32, name=f"bank{2 * n}"), psum.tile([P, PM], F32, name=f"bank{2 * n + 1}"))
-            for n in range(ntiles)
+            for n in range(OUT_TILES)
         ]
 
         def second_products(b, n):
             cols = slice(n * P, (n + 1) * P)
-            zc, zs = z_q[b]
+            z_words, z_scales = z_q[b]
             codes, scales = w3_q[b]
             nc.tensor.matmul_mx(
                 out=acc[n][0][:], lhsT=codes[:, cols].bitcast(FP8X4), lhsT_scale=scales[:, cols],
-                rhs=zc[:].bitcast(FP8X4), rhs_scale=zs[:], start=(b == 0), stop=(b == rp - 1),
+                rhs=z_words.bitcast(FP8X4), rhs_scale=z_scales[:], start=(b == 0), stop=(b == R_PASSES - 1),
             )
             nc.tensor.matmul_mx(
                 out=acc[n][1][:], lhsT=w4_w[:, b, cols].bitcast(FP8X4), lhsT_scale=w4_s[:, b, cols],
-                rhs=zc[:].bitcast(FP8X4), rhs_scale=zs[:], start=(b == 0), stop=(b == rp - 1),
+                rhs=z_words.bitcast(FP8X4), rhs_scale=z_scales[:], start=(b == 0), stop=(b == R_PASSES - 1),
             )
 
-        for n in range(ntiles):
+        for n in range(OUT_TILES):
             second_products(0, n)
-        z_q[1] = quantise(z_last[:].rearrange("p m i -> p (m i)"), PM, "z1")
-        for n in range(ntiles):
+        z_codes = held([P, PM], U32, "z_codes1")
+        z_q[1] = quantise(z_codes[:], z_dealt[:].rearrange("p m i -> p (m i)"), "z_scales1")
+        for n in range(OUT_TILES):
             second_products(1, n)
-        for n in range(ntiles):
-            audited = held([P, PM], F32, f"edit{n}")
+        for n in range(OUT_TILES):
+            audited = held([P, PM], F32, f"audited{n}", slot=f"edit{n}")
             nc.vector.tensor_tensor(out=audited[:], in0=acc[n][0][:], in1=audit_t[n], op=ALU.mult)
-            result = ring.tile([P, PM], F32, name="result", bufs=4)
-            if n < TAIL_G:
-                fourth = ring.tile([P, PM], F32, name="second", bufs=2)
-                nc.scalar.copy(out=fourth[:], in_=acc[n][1][:])
-                nc.gpsimd.tensor_tensor(out=result[:], in0=fourth[:], in1=audited[:], op=ALU.add)
+            result = ring.tile([P, PM], F32, name="result", bufs=OUT_TILES)
+            if n < POOL_OUT:
+                by_w4 = ring.tile([P, PM], F32, name="by_w4", bufs=POOL_OUT)
+                nc.scalar.copy(out=by_w4[:], in_=acc[n][1][:])
+                nc.gpsimd.tensor_tensor(out=result[:], in0=by_w4[:], in1=audited[:], op=ALU.add)
             else:
                 nc.vector.tensor_tensor(out=result[:], in0=acc[n][1][:], in1=audited[:], op=ALU.add)
             nc.sync.dma_start(out=out[n * P : (n + 1) * P, :], in_=result[:])

@@ -43,7 +43,7 @@ def tile_list_repair_error_scores_kernel(
     with ExitStack() as ctx:
         lists = ctx.enter_context(tc.tile_pool(name="lists", bufs=1))
         keep = ctx.enter_context(tc.tile_pool(name="keep", bufs=1))
-        ring = ctx.enter_context(tc.tile_pool(name="ring", bufs=3))
+        ring = ctx.enter_context(tc.tile_pool(name="ring", bufs=2))
         psum = ctx.enter_context(tc.psum_pool(name="psum", bufs=1))
 
         def held(shape, dtype, name, slot=None):
@@ -74,9 +74,8 @@ def tile_list_repair_error_scores_kernel(
             rows = w1[a * PASS : (a + 1) * PASS, u0 * P : u1 * P]
             nc.sync.dma_start(out=raw[:], in_=rows.rearrange("(p j) c -> p j c", j=PACK))
 
-        def load_w1_plain(u0, u1):
-            for a in range(K_PASSES):
-                load_w1_rows(held([P, PACK, (u1 - u0) * P], F32, f"w1_raw{a}{u0}"), a, u0, u1)
+        def load_w1_plain(a, u0, u1):
+            load_w1_rows(held([P, PACK, (u1 - u0) * P], F32, f"w1_raw{a}{u0}"), a, u0, u1)
 
         def load_w1_dealt():
             load_w1_rows(ring.tile([P, PACK, PASS], F32, name="raw", bufs=2), 0, PLAIN, TILES)
@@ -154,8 +153,9 @@ def tile_list_repair_error_scores_kernel(
             wgs_t[u] = wgs_plain[:]
 
         nc.sync.dma_start(idx[:], offs)
-        load_w1_plain(0, 2)
+        load_w1_plain(0, 0, 2)
         load_scales(tab_s, tab_scales)
+        load_w1_plain(1, 0, 2)
         load_tab(0)
         load_tab(1)
         load_scales(w2_s, w2_scales)
@@ -167,7 +167,8 @@ def tile_list_repair_error_scores_kernel(
         load_vectors_plain()
         load_edit_plain(1)
         nc.sync.dma_start(idx3[:], offs3)
-        load_w1_plain(2, PLAIN)
+        load_w1_plain(0, 2, PLAIN)
+        load_w1_plain(1, 2, PLAIN)
         load_edit_plain(2)
         load_edit_plain(3)
         load_page(1)
@@ -233,14 +234,18 @@ def tile_list_repair_error_scores_kernel(
                     cols = slice(a * width + (u - u0) * P, a * width + (u - u0 + 1) * P)
                     w1_q[a, u] = (codes[:, cols], scales[:, cols])
 
-        def prepare_w1_dealt(a, grouped, codes):
-            nc.scalar.copy(
-                out=grouped[:].rearrange("p (i m j) -> p m j i", i=PACK, j=PACK),
-                in_=w1_raw[a, PLAIN][:].rearrange("p j (m i) -> p m j i", i=PACK),
-            )
-            codes, scales = quantise(codes, grouped[:], f"w1_scales_dealt{a}")
-            for i in range(PACK):
-                w1_q[a, PLAIN + i] = (codes[:, i * P : (i + 1) * P], scales[:, i * P : (i + 1) * P])
+        def prepare_w1_dealt(codes):
+            grouped = held([P, K_PASSES, PASS * PACK], BF16, "grouped_dealt")
+            for a in range(K_PASSES):
+                nc.scalar.copy(
+                    out=grouped[:, a, :].rearrange("p (i m j) -> p m j i", i=PACK, j=PACK),
+                    in_=w1_raw[a, PLAIN][:].rearrange("p j (m i) -> p m j i", i=PACK),
+                )
+            codes, scales = quantise(codes, grouped[:].rearrange("p a c -> p (a c)"), "w1_scales_dealt")
+            for a in range(K_PASSES):
+                for i in range(PACK):
+                    cols = slice(a * PASS + i * P, a * PASS + (i + 1) * P)
+                    w1_q[a, PLAIN + i] = (codes[:, cols], scales[:, cols])
 
         w2_w_dealt = held([P, K_PASSES, 2 * PASS], U8, "w2_w_dealt")
         w2_s_dealt = held([P, K_PASSES, PASS], U8, "w2_s_dealt")
@@ -327,7 +332,7 @@ def tile_list_repair_error_scores_kernel(
                 nc.vector.tensor_copy(page[u][:].indirect(idx2[:]), to_put[u][:])
 
         def row_bias(u):
-            scratch = held([P, T2], F32, f"scratch{u}", slot="scratch" if u < FUSED else "grouped_last")
+            scratch = held([P, T2], F32, f"scratch{u}", slot="scratch" if u < FUSED else "grouped_dealt")
             nc.vector.tensor_scalar(
                 out=scratch[:], in0=page[u][:], scalar1=column(neg_temp, u), scalar2=None,
                 op0=ALU.mult, op1=ALU.min, accum_out=bias[:, u : u + 1],
@@ -397,10 +402,8 @@ def tile_list_repair_error_scores_kernel(
         prepare_tile(3)
 
         put(2)
-        w1_codes = held([P, K_PASSES, PASS], U32, "w1_codes_dealt", slot="to_put2")
-        grouped_first = ring.tile([P, PASS * PACK], BF16, name="grouped", align_bytes=64)
-        prepare_w1_dealt(0, grouped_first, w1_codes[:, 0, :])
-        prepare_w1_dealt(1, held([P, PASS * PACK], BF16, "grouped_last"), w1_codes[:, 1, :])
+        w1_codes = held([P, K_PASSES * PASS], U32, "w1_codes_dealt", slot="to_put2")
+        prepare_w1_dealt(w1_codes[:])
         deal_w2_words()
         row_bias(2)
         prepare_tile(PLAIN)
@@ -413,13 +416,13 @@ def tile_list_repair_error_scores_kernel(
             if u == LAST:
                 z_codes = held([P, PM], U32, "z_codes0", slot=f"to_put{u}")
                 z_q[0] = quantise(z_codes[:], z_grouped[:], "z_scales0")
+            if u + 2 < TILES:
+                prepare_tile(u + 2)
+            row_bias(u)
             if u == LAST - 1:
                 w3_codes = held([P, R_PASSES, N], U32, "w3_codes", slot=f"to_put{u}")
                 for b in range(R_PASSES):
                     w3_q[b] = quantise(w3_codes[:, b, :], w3_grouped[b][:], f"w3_scales{b}")
-            if u + 2 < TILES:
-                prepare_tile(u + 2)
-            row_bias(u)
             look(u)
             if u == PLAIN - 1:
                 round_w3(1)

from contextlib import ExitStack

import concourse.mybir as mybir
from concourse.masks import make_identity

K, T, S, T2, PM, H, N = 1024, 2048, 512, 1024, 512, 1024, 512
FLOPS = 2 * 2 * K * H * S + 2 * 2 * H * N * PM

F32 = mybir.dt.float32
BF16 = mybir.dt.bfloat16
I32 = mybir.dt.int32
U32 = mybir.dt.uint32
U16 = mybir.dt.uint16
U8 = mybir.dt.uint8
FP8X4 = mybir.dt.float8_e4m3fn_x4
FP4X4 = mybir.dt.float4_e2m1fn_x4
ALU = mybir.AluOpType
ACT = mybir.ActivationFunctionType

P = 128
PACK = 4
PASS = P * PACK
K_PASSES = K // PASS
R_PASSES = H // PASS
TILES = H // P
PLAIN = PACK
LAST = TILES - 1
OUT_TILES = N // P
QUADRANTS = (0, 2, 1, 3)

FUSED = 2
POOL_SUM = 3
POOL_EDIT = 6
POOL_OUT = 2


def tile_list_repair_error_scores_kernel(
    tc, tab_words, tab_scales, offs, w1, w2_words, w2_scales, edit, page0, wgs,
    offs2, offs3, temp, gain, w3, w4_words, w4_scales, audit, out,
):
    nc = tc.nc

    with ExitStack() as ctx:
        lists = ctx.enter_context(tc.tile_pool(name="lists", bufs=1))
        keep = ctx.enter_context(tc.tile_pool(name="keep", bufs=1))
        ring = ctx.enter_context(tc.tile_pool(name="ring", bufs=2))
        psum = ctx.enter_context(tc.psum_pool(name="psum", bufs=1))

        def held(shape, dtype, name, slot=None):
            return keep.tile(shape, dtype, name=name, tag=slot or name, align_bytes=64)

        idx = lists.tile([P, S // 16], U16, name="idx")
        idx2 = lists.tile([P, S // 16], U16, name="idx2")
        idx3 = lists.tile([P, PM // 16], U16, name="idx3")

        tab_s = held([P, K_PASSES, T], U8, "tab_s")
        w2_s = held([P, K_PASSES, H], U8, "w2_s")
        w4_s = held([P, R_PASSES, N], U8, "w4_s")
        nc.vector.memset(tab_s[:].rearrange("p a t -> p (a t)").bitcast(I32), 0)
        nc.gpsimd.memset(w2_s[:].rearrange("p a t -> p (a t)").bitcast(I32), 0)
        nc.vector.memset(w4_s[:].rearrange("p a t -> p (a t)").bitcast(I32), 0)

        w1_raw, w2_w, tab_w, w3_raw, edit_t, page, wgs_t, audit_t = {}, {}, {}, {}, {}, {}, {}, {}

        def load_scales(tile, src):
            for q in QUADRANTS:
                nc.sync.dma_start(
                    out=tile[32 * q : 32 * q + 4].bitcast(I32),
                    in_=src[:, 4 * q : 4 * q + 4, :].rearrange("a r c -> r a c").bitcast(I32),
                )

        def load_w1_rows(raw, a, u0, u1):
            w1_raw[a, u0] = raw
            rows = w1[a * PASS : (a + 1) * PASS, u0 * P : u1 * P]
            nc.sync.dma_start(out=raw[:], in_=rows.rearrange("(p j) c -> p j c", j=PACK))

        def load_w1_plain(a, u0, u1):
            load_w1_rows(held([P, PACK, (u1 - u0) * P], F32, f"w1_raw{a}{u0}"), a, u0, u1)

        def load_w1_dealt():
            load_w1_rows(ring.tile([P, PACK, PASS], F32, name="raw", bufs=2), 0, PLAIN, TILES)
            load_w1_rows(held([P, PACK, PASS], F32, "w1_raw_last"), 1, PLAIN, TILES)

        def load_w2(half):
            w2_w[half] = held([P, K_PASSES, 2 * PASS], U8, f"w2_w{half}")
            src = w2_words[:, :, 2 * half * PASS : 2 * (half + 1) * PASS]
            nc.sync.dma_start(out=w2_w[half][:].bitcast(I32), in_=src.rearrange("a p c -> p a c").bitcast(I32))

        def load_tab(a):
            tab_w[a] = held([P, T], U32, f"tab_w{a}")
            nc.sync.dma_start(
                out=tab_w[a][:].bitcast(I32),
                in_=tab_words[a].rearrange("p t i -> p (t i)").bitcast(I32),
            )

        def load_edit_plain(u):
            edit_t[u] = held([P, S], F32, f"edit{u}")
            nc.sync.dma_start(out=edit_t[u][:], in_=edit[u * P : (u + 1) * P, :])

        def load_edit_dealt():
            tile = held([P, PACK, S], F32, "edit_dealt")
            nc.sync.dma_start(out=tile[:], in_=edit[PASS:, :].rearrange("(p i) j -> p i j", i=PACK))
            for i in range(PACK):
                edit_t[PLAIN + i] = tile[:, i, :]

        def load_page(u):
            page[u] = held([P, T2], F32, f"page{u}")
            if u < PLAIN:
                rows = page0[u * P : (u + 1) * P, :]
            else:
                rows = page0[PASS:, :].rearrange("(p i) c -> i p c", i=PACK)[u - PLAIN]
            nc.sync.dma_start(out=page[u][:], in_=rows)

        def load_wgs_dealt():
            tile = held([P, PACK, S], F32, "wgs_dealt")
            for q in QUADRANTS:
                nc.sync.dma_start(out=tile[32 * q : 32 * q + 32], in_=wgs.rearrange("(q i) j -> q i j", i=PACK))
            for i in range(PACK):
                wgs_t[PLAIN + i] = tile[:, i, :]

        def load_w3(b):
            w3_raw[b] = ring.tile([P, PACK, N], F32, name="raw", bufs=2)
            nc.sync.dma_start(
                out=w3_raw[b][:],
                in_=w3[b * PASS : (b + 1) * PASS, :].rearrange("(p j) c -> p j c", j=PACK),
            )

        def load_audit():
            tile = held([P, OUT_TILES, PM], F32, "audit", slot="z_plain")
            nc.sync.dma_start(out=tile[:], in_=audit.rearrange("(n p) m -> p n m", p=P))
            for n in range(OUT_TILES):
                audit_t[n] = tile[:, n, :]

        vec_rows = held([P, P], F32, "vec_rows")
        identity = held([P, P], F32, "identity")
        nc.gpsimd.memset(vec_rows[:], 0.0)
        make_identity(nc, identity[:])
        plain_cols = held([P, 2 * PLAIN], F32, "plain_cols")
        temp_t = [plain_cols[:, :PLAIN], held([P, PACK], F32, "temp_dealt")]
        gain_t = [plain_cols[:, PLAIN:], held([P, PACK], F32, "gain_dealt")]

        def load_vectors_plain():
            for at, vec in ((0, temp), (PLAIN, gain)):
                nc.sync.dma_start(out=vec_rows[at : at + PLAIN, :], in_=vec[:PASS].rearrange("(u p) -> u p", p=P))

        def load_vectors_dealt():
            for tile, vec in ((temp_t[1], temp), (gain_t[1], gain)):
                nc.sync.dma_start(out=tile[:], in_=vec[PASS:].rearrange("(p i) -> p i", i=PACK))

        wgs_plain = held([P, S], F32, "wgs_plain")
        w4_w = held([P, R_PASSES, N], U32, "w4_w")
        for u in range(PLAIN):
            wgs_t[u] = wgs_plain[:]

        nc.sync.dma_start(idx[:], offs)
        load_w1_plain(0, 0, 2)
        load_scales(tab_s, tab_scales)
        load_w1_plain(1, 0, 2)
        load_tab(0)
        load_tab(1)
        load_scales(w2_s, w2_scales)
        load_w2(0)
        load_edit_plain(0)
        nc.sync.dma_start(out=wgs_plain[:], in_=wgs)
        nc.sync.dma_start(idx2[:], offs2)
        load_page(0)
        load_vectors_plain()
        load_edit_plain(1)
        nc.sync.dma_start(idx3[:], offs3)
        load_w1_plain(0, 2, PLAIN)
        load_w1_plain(1, 2, PLAIN)
        load_edit_plain(2)
        load_edit_plain(3)
        load_page(1)
        load_w2(1)
        load_w1_dealt()
        load_page(2)
        load_edit_dealt()
        load_w3(0)
        load_page(3)
        load_wgs_dealt()
        load_vectors_dealt()
        load_page(4)
        load_w3(1)
        load_page(5)
        load_scales(w4_s, w4_scales)
        nc.sync.dma_start(
            out=w4_w[:].bitcast(I32),
            in_=w4_words.rearrange("a p c i -> p a (c i)").bitcast(I32),
        )
        load_page(6)
        load_page(LAST)

        turned = psum.tile([P, P], F32, name="bank7")
        nc.tensor.transpose(turned[:], vec_rows[:], identity[:])
        nc.scalar.copy(out=plain_cols[:], in_=turned[:, : 2 * PLAIN])
        neg_temp = [held([P, PACK], F32, f"neg_temp{half}") for half in range(R_PASSES)]
        for half in range(R_PASSES):
            nc.scalar.mul(neg_temp[half][:], temp_t[half][:], -1.0)

        def column(halves, u):
            return halves[u // PACK][:, u % PACK : u % PACK + 1]

        v_s, v_w, w1_q, w3_grouped, w3_q, z_q = {}, {}, {}, {}, {}, {}

        def gather_scales(a):
            v_s[a] = held([P, S], U8, f"v_s{a}")
            nc.vector.tensor_copy(v_s[a][:], tab_s[:, a, :].indirect(idx[:]))

        def gather_words(a):
            v_w[a] = held([P, S], U32, f"v_w{a}")
            nc.vector.tensor_copy(v_w[a][:], tab_w[a][:].indirect(idx[:]))

        def quantise(codes, grouped, name):
            scales = held([P, codes.shape[1]], U8, name)
            nc.vector.quantize_mx(out=codes.bitcast(FP8X4), scales=scales[:], in_=grouped)
            return codes, scales

        def interleave(grouped, rows):
            nc.scalar.copy(
                out=grouped.rearrange("p (c e j) -> p c j e", e=4, j=PACK),
                in_=rows.rearrange("p j (c e) -> p c j e", e=4),
            )

        def prepare_w1_plain(u0, u1):
            width = (u1 - u0) * P
            grouped = ring.tile([P, K_PASSES, width * PACK], BF16, name="grouped", align_bytes=64)
            for a in range(K_PASSES):
                interleave(grouped[:, a, :], w1_raw[a, u0][:])
            codes = held([P, K_PASSES * width], U32, f"w1_codes{u0}")
            codes, scales = quantise(codes[:], grouped[:].rearrange("p a c -> p (a c)"), f"w1_scales{u0}")
            for a in range(K_PASSES):
                for u in range(u0, u1):
                    cols = slice(a * width + (u - u0) * P, a * width + (u - u0 + 1) * P)
                    w1_q[a, u] = (codes[:, cols], scales[:, cols])

        def prepare_w1_dealt(codes):
            grouped = held([P, K_PASSES, PASS * PACK], BF16, "grouped_dealt")
            for a in range(K_PASSES):
                nc.scalar.copy(
                    out=grouped[:, a, :].rearrange("p (i m j) -> p m j i", i=PACK, j=PACK),
                    in_=w1_raw[a, PLAIN][:].rearrange("p j (m i) -> p m j i", i=PACK),
                )
            codes, scales = quantise(codes, grouped[:].rearrange("p a c -> p (a c)"), "w1_scales_dealt")
            for a in range(K_PASSES):
                for i in range(PACK):
                    cols = slice(a * PASS + i * P, a * PASS + (i + 1) * P)
                    w1_q[a, PLAIN + i] = (codes[:, cols], scales[:, cols])

        w2_w_dealt = held([P, K_PASSES, 2 * PASS], U8, "w2_w_dealt")
        w2_s_dealt = held([P, K_PASSES, PASS], U8, "w2_s_dealt")

        def deal_w2_scales():
            nc.vector.tensor_copy(
                out=w2_s_dealt[:].rearrange("p a (i m) -> p a i m", i=PACK),
                in_=w2_s[:, :, PASS:].rearrange("p a (m i) -> p a i m", i=PACK),
            )

        def deal_w2_words():
            nc.scalar.copy(
                out=w2_w_dealt[:].bitcast(U16).rearrange("p a (i m) -> p a i m", i=PACK),
                in_=w2_w[1][:].bitcast(U16).rearrange("p a (m i) -> p a i m", i=PACK),
            )

        def round_w3(b):
            w3_grouped[b] = ring.tile([P, N * PACK], BF16, name="grouped", align_bytes=64)
            interleave(w3_grouped[b][:], w3_raw[b][:])

        bias = held([P, TILES], F32, "bias")
        z_plain = held([P, PLAIN, PM], F32, "z_plain")
        z_dealt = held([P, PM, PACK], BF16, "z_dealt")
        banks, edited, to_put = {}, {}, {}

        def first_products(u):
            i = u % PACK
            words, scale_bytes = (w2_w[0], w2_s) if u < PLAIN else (w2_w_dealt, w2_s_dealt)
            by_w1 = psum.tile([P, S], F32, name=f"bank{2 * i}")
            by_w2 = psum.tile([P, S], F32, name=f"bank{2 * i + 1}")
            for a in range(K_PASSES):
                codes, scales = w1_q[a, u]
                nc.tensor.matmul_mx(
                    out=by_w1[:], lhsT=codes.bitcast(FP8X4), lhsT_scale=scales,
                    rhs=v_w[a][:].bitcast(FP8X4), rhs_scale=v_s[a][:],
                    start=(a == 0), stop=(a == K_PASSES - 1),
                )
            for a in range(K_PASSES):
                nc.tensor.matmul_mx(
                    out=by_w2[:], lhsT=words[:, a, 2 * i * P : 2 * (i + 1) * P].bitcast(FP4X4),
                    lhsT_scale=scale_bytes[:, a, i * P : (i + 1) * P],
                    rhs=v_w[a][:].bitcast(FP8X4), rhs_scale=v_s[a][:],
                    start=(a == 0), stop=(a == K_PASSES - 1),
                )
            banks[u] = (by_w1, by_w2)

        def times_edit(u):
            if u >= POOL_EDIT:
                by_w1 = held([P, S], F32, f"by_w1_{u}", slot="w2_w0" if u == LAST else None)
                nc.scalar.copy(out=by_w1[:], in_=banks[u][0][:])
                edited[u] = held([P, S], F32, f"edited{u}", slot="h")
                nc.gpsimd.tensor_tensor(out=edited[u][:], in0=by_w1[:], in1=edit_t[u][:], op=ALU.mult)
            else:
                edited[u] = held([P, S], F32, f"edited{u}", slot=f"to_put{u - 2}") if u > PLAIN else edit_t[u]
                nc.vector.tensor_tensor(out=edited[u][:], in0=banks[u][0][:], in1=edit_t[u][:], op=ALU.mult)

        def sum_products(u):
            if u >= POOL_EDIT:
                h = edited[u]
            else:
                h = held([P, S], F32, f"h{u}", slot=f"to_put{u}" if u < FUSED else "h")
            if u >= POOL_SUM:
                spent_w1 = f"w1_raw{u % 2}{2 * ((u - PLAIN) // 2)}"
                by_w2 = held([P, S], F32, f"by_w2_{u}", slot=spent_w1 if u >= PLAIN else None)
                nc.scalar.copy(out=by_w2[:], in_=banks[u][1][:])
                nc.gpsimd.tensor_tensor(out=h[:], in0=by_w2[:], in1=edited[u][:], op=ALU.add)
            else:
                nc.vector.tensor_tensor(out=h[:], in0=banks[u][1][:], in1=edited[u][:], op=ALU.add)
            return h

        def weigh(u):
            h = sum_products(u)
            if u < FUSED:
                to_put[u] = h
            else:
                to_put[u] = held([P, S], F32, f"to_put{u}")
                engine = nc.gpsimd if u >= POOL_SUM else nc.vector
                engine.tensor_tensor(out=to_put[u][:], in0=h[:], in1=wgs_t[u], op=ALU.mult)

        def put(u):
            if u < FUSED:
                nc.vector.tensor_tensor(page[u][:].indirect(idx2[:]), to_put[u][:], wgs_t[u], ALU.mult)
            else:
                nc.vector.tensor_copy(page[u][:].indirect(idx2[:]), to_put[u][:])

        def row_bias(u):
            scratch = held([P, T2], F32, f"scratch{u}", slot="scratch" if u < FUSED else "grouped_dealt")
            nc.vector.tensor_scalar(
                out=scratch[:], in0=page[u][:], scalar1=column(neg_temp, u), scalar2=None,
                op0=ALU.mult, op1=ALU.min, accum_out=bias[:, u : u + 1],
            )

        def look(u):
            slot = "w1_raw12" if u == 0 else "z_back" if u >= LAST - 1 else "w1_raw_last"
            x = held([P, PM], F32, f"x{u}", slot=slot)
            parts = 2 if u == LAST else 1
            width = PM // parts
            for part in range(parts):
                cols = slice(part * width, (part + 1) * width)
                entries = idx3[:, part * width // 16 : (part + 1) * width // 16]
                nc.scalar.activation(
                    out=x[:, cols], in_=page[u][:].indirect(entries), func=ACT.Exp,
                    bias=bias[:, u : u + 1], scale=column(temp_t, u),
                )
                if u < PLAIN:
                    nc.scalar.activation(out=z_plain[:, u, :], in_=x[:, cols], func=ACT.Copy, scale=column(gain_t, u))
                elif u < LAST:
                    nc.scalar.activation(
                        out=z_dealt[:, cols, u - PLAIN], in_=x[:, cols], func=ACT.Copy, scale=column(gain_t, u),
                    )
                else:
                    nc.vector.tensor_scalar(
                        out=z_dealt[:, cols, u - PLAIN], in0=x[:, cols],
                        scalar1=column(gain_t, u), scalar2=None, op0=ALU.mult,
                    )

        def regroup_plain_z():
            parked = out.rearrange("(u p) m -> p u m", p=P)
            for u0, u1 in ((0, PLAIN - 1), (PLAIN - 1, PLAIN)):
                nc.sync.dma_start(out=parked[:, u0:u1, :], in_=z_plain[:, u0:u1, :])
            z_back = held([P, PACK, PM], F32, "z_back")
            nc.sync.dma_start(out=z_back[:], in_=out.rearrange("(p i) m -> p i m", i=PACK))
            grouped = held([P, PM * PACK], BF16, "z_grouped")
            interleave(grouped[:], z_back[:])
            return grouped

        def prepare_tile(u):
            if u >= PLAIN:
                first_products(u)
            times_edit(u)
            weigh(u)

        prepare_w1_plain(0, 2)
        for a in range(K_PASSES):
            gather_scales(a)
        for a in range(K_PASSES):
            gather_words(a)
        first_products(0)
        first_products(1)
        prepare_tile(0)
        deal_w2_scales()

        put(0)
        row_bias(0)
        prepare_tile(1)
        prepare_w1_plain(2, PLAIN)
        first_products(2)
        first_products(3)
        look(0)

        put(1)
        row_bias(1)
        prepare_tile(2)
        prepare_tile(3)

        put(2)
        w1_codes = held([P, K_PASSES * PASS], U32, "w1_codes_dealt", slot="to_put2")
        prepare_w1_dealt(w1_codes[:])
        deal_w2_words()
        row_bias(2)
        prepare_tile(PLAIN)
        look(1)
        look(2)
        round_w3(0)

        for u in range(3, TILES):
            put(u)
            if u == LAST:
                z_codes = held([P, PM], U32, "z_codes0", slot=f"to_put{u}")
                z_q[0] = quantise(z_codes[:], z_grouped[:], "z_scales0")
            if u + 2 < TILES:
                prepare_tile(u + 2)
            row_bias(u)
            if u == LAST - 1:
                w3_codes = held([P, R_PASSES, N], U32, "w3_codes", slot=f"to_put{u}")
                for b in range(R_PASSES):
                    w3_q[b] = quantise(w3_codes[:, b, :], w3_grouped[b][:], f"w3_scales{b}")
            look(u)
            if u == PLAIN - 1:
                round_w3(1)
            if u == PLAIN:
                z_grouped = regroup_plain_z()
                load_audit()

        acc = [
            (psum.tile([P, PM], F32, name=f"bank{2 * n}"), psum.tile([P, PM], F32, name=f"bank{2 * n + 1}"))
            for n in range(OUT_TILES)
        ]

        def second_products(b, n):
            cols = slice(n * P, (n + 1) * P)
            z_words, z_scales = z_q[b]
            codes, scales = w3_q[b]
            nc.tensor.matmul_mx(
                out=acc[n][0][:], lhsT=codes[:, cols].bitcast(FP8X4), lhsT_scale=scales[:, cols],
                rhs=z_words.bitcast(FP8X4), rhs_scale=z_scales[:], start=(b == 0), stop=(b == R_PASSES - 1),
            )
            nc.tensor.matmul_mx(
                out=acc[n][1][:], lhsT=w4_w[:, b, cols].bitcast(FP8X4), lhsT_scale=w4_s[:, b, cols],
                rhs=z_words.bitcast(FP8X4), rhs_scale=z_scales[:], start=(b == 0), stop=(b == R_PASSES - 1),
            )

        for n in range(OUT_TILES):
            second_products(0, n)
        z_codes = held([P, PM], U32, "z_codes1")
        z_q[1] = quantise(z_codes[:], z_dealt[:].rearrange("p m i -> p (m i)"), "z_scales1")
        for n in range(OUT_TILES):
            second_products(1, n)
        for n in range(OUT_TILES):
            audited = held([P, PM], F32, f"audited{n}", slot=f"edit{n}")
            nc.vector.tensor_tensor(out=audited[:], in0=acc[n][0][:], in1=audit_t[n], op=ALU.mult)
            result = ring.tile([P, PM], F32, name="result", bufs=OUT_TILES)
            if n < POOL_OUT:
                by_w4 = ring.tile([P, PM], F32, name="by_w4", bufs=POOL_OUT)
                nc.scalar.copy(out=by_w4[:], in_=acc[n][1][:])
                nc.gpsimd.tensor_tensor(out=result[:], in0=by_w4[:], in1=audited[:], op=ALU.add)
            else:
                nc.vector.tensor_tensor(out=result[:], in0=acc[n][1][:], in1=audited[:], op=ALU.add)
            nc.sync.dma_start(out=out[n * P : (n + 1) * P, :], in_=result[:])
